import numpy as np
import ml_dtypes


def mxq(x, axis, fmt="e4m3"):
    dtype, down = {"e4m3": (ml_dtypes.float8_e4m3fn, 7), "e5m2": (ml_dtypes.float8_e5m2, 14)}[fmt]
    v = np.moveaxis(np.asarray(x, np.float32).astype(ml_dtypes.bfloat16).astype(np.float64), axis, -1)
    blocks = v.reshape(v.shape[:-1] + (-1, 32))
    amax = np.abs(blocks).max(-1, keepdims=True)
    byte = np.maximum(np.where(amax > 0, np.frexp(amax)[1] - 1 + 127, 0) - down, 1)
    scale = np.exp2(byte - 127.0)
    codes = (blocks / scale).astype(np.float32).astype(dtype).astype(np.float64)
    return np.moveaxis((codes * scale).reshape(v.shape), -1, axis)


WIDE = False


def mx_kscale(k):
    if not WIDE:
        return np.ones(k)
    levels = np.array([10, -10, 5, -5, 0])
    if k % 512:
        return np.exp2(np.random.permutation(np.resize(levels, k // 32))).repeat(32)
    a = np.empty((k // 512, 16))
    for p in range(k // 512):
        a[p, :8] = np.random.permutation(np.resize(levels, 8))
        for g in range(8):
            far = levels[np.abs(levels - a[p, g]) >= 10]
            a[p, g + 8] = far[np.random.randint(len(far))]
    return np.exp2(a.ravel()).repeat(32)


BF16 = ml_dtypes.bfloat16


def bf(x):
    return np.asarray(x, np.float32).astype(BF16)


def f64(x):
    return np.asarray(x).astype(np.float64)


F, K, T, TAU = 512, 512, 1024, 4
TK = TAU * K
TF = TAU * F


def softplus(a):
    return np.maximum(a, 0.0) + np.log1p(np.exp(-np.abs(a)))


def delay(x, tau):
    n = x.shape[1]
    return np.concatenate([x[:, n - tau:], x[:, :n - tau]], axis=1)


def advance(x, tau):
    return np.concatenate([x[:, tau:], x[:, :tau]], axis=1)


def draw0():
    s, u = mx_kscale(TK), mx_kscale(TF)
    return {
        "v": bf(np.random.uniform(0.2, 1.8, (F, T))),
        "h": bf(np.random.uniform(0.2, 1.8, (K, T))),
        "w1": bf(np.random.standard_normal((F, TK)) / np.sqrt(TK) / s[None, :]),
        "g1": bf(np.random.standard_normal(TK) * s),
        "w2": bf(np.random.standard_normal((K, TF)) * 1.5 / np.sqrt(TF) / u[None, :]),
        "g2": bf((1.0 + 0.2 * np.random.standard_normal(TF)) * u),
        "mu": bf(np.random.uniform(0.1, 0.5, K)),
    }


def core(v, h, w1, g1, w2, g2, mu):
    v, h, w1, g1, w2, g2, mu = f64(v), f64(h), f64(w1), f64(g1), f64(w2), f64(g2), f64(mu)
    hs = np.concatenate([delay(h, tau) for tau in range(TAU)], axis=0)
    hg = g1[:, None] * hs
    s = mxq(w1, 1, "e4m3") @ mxq(hg, 0, "e4m3")
    e = v / (softplus(s) + 0.25) - 1.0
    es = np.concatenate([advance(e, tau) for tau in range(TAU)], axis=0)
    eg = g2[:, None] * es
    r = mxq(w2, 1, "e4m3") @ mxq(eg, 0, "e4m3")
    return h * np.exp(0.5 * (r - mu[:, None]))


def e4m3fn_bytes(y):
    return np.clip(np.asarray(y, np.float64), -448.0, 448.0).astype(np.float32).astype(ml_dtypes.float8_e4m3fn).view(np.uint8)


def e4m3fn_values(b):
    return np.asarray(b, np.uint8).view(ml_dtypes.float8_e4m3fn).astype(np.float64)


def setup_inputs():
    d = draw0()
    x0 = np.asarray(d['w2']).astype(np.float64)
    s = (np.max(np.abs(x0), axis=(0,), keepdims=True) / 448.0).astype(np.float32)
    out = {}
    for k, v in d.items():
        if k == 'w2':
            out['w2_bytes'] = e4m3fn_bytes(x0 / s.astype(np.float64))
            out['w2_scale'] = s
        else:
            out[k] = v
    return out


def reference(v, h, w1, g1, w2_bytes, w2_scale, g2, mu):
    return core(v, h, w1, g1, e4m3fn_values(w2_bytes) * w2_scale.astype(np.float64), g2, mu)

@@ -1,0 +1,392 @@
+from contextlib import ExitStack
+
+import concourse.mybir as mybir
+from concourse.masks import make_identity
+
+F32 = mybir.dt.float32
+BF16 = mybir.dt.bfloat16
+U32 = mybir.dt.uint32
+U8 = mybir.dt.uint8
+FP8 = mybir.dt.float8_e4m3fn
+FP8X4 = mybir.dt.float8_e4m3fn_x4
+ALU = mybir.AluOpType
+ACT = mybir.ActivationFunctionType
+
+F, K, T, TAU = 512, 512, 1024, 4
+P = 128
+FLOPS = 2 * 2 * F * TAU * K * T
+
+HALF = 512
+TINY = 2.0 ** -60
+CHUNKS = ((0, 384), (384, 768), (768, T))
+
+
+def tile_convolutivenmfexponentiatedupdate_kernel(tc, v, h, w1, g1, w2_bytes, w2_scale, g2, mu, out):
+    nc = tc.nc
+    with ExitStack() as ctx:
+        ctx.enter_context(tc.manual_schedule())
+        keep = ctx.enter_context(tc.tile_pool(name="keep", bufs=1))
+        stage = ctx.enter_context(tc.tile_pool(name="stage", bufs=3))
+        psum = ctx.enter_context(tc.psum_pool(name="psum", bufs=1))
+
+        def bank(i):
+            return psum.tile([P, 512], F32, name="bank%d" % i, tag="bank%d" % i)
+
+        def bank16(i):
+            return psum.tile([P, 4, 256], BF16, name="bank%d" % i, tag="bank%d" % i)
+
+        h_sb = keep.tile([P, 4, 16 + T], BF16, name="h_sb", align_bytes=64)
+        w1_sb = keep.tile([P, 4, TAU * K], BF16, name="w1_sb", tag="rows", align_bytes=64)
+        v_sb = keep.tile([P, 4, T], BF16, name="v_sb")
+        w2_by = keep.tile([P, 4, TAU * F], U8, name="w2_by", align_bytes=64)
+        sc_sb = keep.tile([P, TAU * F], F32, name="sc_sb", align_bytes=64)
+        g1_sb = keep.tile([P, TAU, 16], BF16, name="g1_sb")
+        g2_sb = keep.tile([P, TAU, 16], BF16, name="g2_sb")
+        mu_sb = keep.tile([P, 16], BF16, name="mu_sb")
+        h_v = h.rearrange("(p j) t -> p j t", j=4)
+        v_v = v.rearrange("(p j) t -> p j t", j=4)
+        w1_v = w1.rearrange("(m b) k -> m b k", b=4)
+        w2_v = w2_bytes.rearrange("(m b) k -> m b k", b=4)
+        nc.scalar.dma_start(out=g1_sb[:, :, 0:4], in_=g1.rearrange("(a p j) -> p a j", a=TAU, j=4))
+        nc.sync.dma_start(out=h_sb[:, :, 12:528], in_=h_v[:, :, 508:T])
+        for g in range(TAU):
+            nc.sync.dma_start(out=w1_sb[:, :, g * 512 : (g + 1) * 512], in_=w1_v[:, :, g * 512 : (g + 1) * 512])
+            if g == 1:
+                nc.sync.dma_start(out=h_sb[:, :, 528:1040], in_=h_v[:, :, 0:512])
+        for b in range(0, 4, 2):
+            nc.sync.dma_start(out=w2_by[:, b : b + 2, :], in_=w2_v[:, b : b + 2, :])
+        nc.sync.dma_start(out=sc_sb[:], in_=w2_scale.rearrange("o k -> (o k)").partition_broadcast(P))
+        nc.sync.dma_start(out=v_sb[:, :, 0:512], in_=v_v[:, :, 512:T])
+        nc.sync.dma_start(out=v_sb[:, :, 512:T], in_=v_v[:, :, 0:512])
+        nc.scalar.dma_start(out=g2_sb[:, :, 0:4], in_=g2.rearrange("(a p j) -> p a j", a=TAU, j=4))
+        nc.scalar.dma_start(out=mu_sb[:, 0:4], in_=mu.rearrange("(p j) -> p j", j=4))
+
+        ident16 = keep.tile([P, P], BF16, name="ident16")
+        make_identity(nc, ident16[:])
+        ident = keep.tile([P, P], F32, name="ident")
+        make_identity(nc, ident[:])
+        dummy = keep.tile([P, 2], F32, name="dummy")
+        nc.vector.memset(dummy[:], 0.0)
+        nc.scalar.activation(out=dummy[:, 1:2], in_=dummy[:, 0:1], func=ACT.Sigmoid)
+
+        g1n = keep.tile([P, TAU, 4], BF16, name="g1n")
+        nc.vector.tensor_scalar(out=g1n[:], in0=g1_sb[:, :, 0:4], scalar1=-1.0, scalar2=None, op0=ALU.mult)
+        diag = keep.tile([P, TAU, 4, P], BF16, name="diag")
+        for tau in range(1, TAU):
+            for j in range(4):
+                nc.vector.tensor_scalar(out=diag[:, tau, j, :], in0=ident16[:], scalar1=g1n[:, tau, j : j + 1], scalar2=None, op0=ALU.mult)
+
+        hg_c = keep.tile([P, TAU, T], U32, name="hg_c", align_bytes=64)
+        hg_s = keep.tile([P, TAU, T], U8, name="hg_s", align_bytes=64)
+        eg_c = keep.tile([P, TAU, T], U32, name="eg_c", align_bytes=64)
+        eg_s = keep.tile([P, TAU, T], U8, name="eg_s", align_bytes=64)
+        w1_c = keep.tile([P, TAU, 512], U32, name="w1_c", align_bytes=64)
+        w1_s = keep.tile([P, TAU, 512], U8, name="w1_s", align_bytes=64)
+        w2_c = keep.tile([P, TAU, 512], U32, name="w2_c", align_bytes=64)
+        w2_s = keep.tile([P, TAU, 512], U8, name="w2_s", align_bytes=64)
+        mid = keep.tile([P, 4, T], F32, name="mid", align_bytes=64)
+        w_il = keep.tile([P, T + 3, 4], F32, name="w_il", align_bytes=64)
+
+        def quantize(codes, scales, grouped):
+            nc.vector.quantize_mx(out=codes.bitcast(FP8X4), scales=scales, in_=grouped)
+
+        wt = {}
+        turned = {}
+        turns = [4]
+
+        def turn(which, src, g, bp, banks):
+            ps = bank(banks[turns[0] % 4])
+            turns[0] += 1
+            turned[(which, g, bp)] = ps
+            words = src.bitcast(F32)
+            for b2 in range(2):
+                for u in range(2):
+                    col = (b2 * 2 + u) * P
+                    nc.tensor.transpose(ps[:, col : col + P], words[:, bp * 2 + b2, 256 * g + u : 256 * (g + 1) : 2], ident[:])
+
+        def empty(copy, which, g, bp):
+            if (which, g) not in wt:
+                wt[(which, g)] = stage.tile([P, 512, 4], BF16, name="wt", align_bytes=64)
+            dst = wt[(which, g)][:, bp * 256 : (bp + 1) * 256, :].rearrange("p m j -> p (m j)").bitcast(F32)
+            copy(
+                out=dst.rearrange("p (b m u) -> p b m u", b=2, u=2),
+                in_=turned[(which, g, bp)][:].rearrange("p (b u m) -> p b m u", b=2, u=2),
+            )
+
+        grp = {}
+
+        def new_grp(key):
+            grp[key] = stage.tile([P, HALF, 4], BF16, name="grouped", align_bytes=64, bufs=8)
+
+        def hg_vector(n, c=None):
+            if (n, 0) not in grp:
+                new_grp((n, 0))
+            a, z = (0, HALF) if c is None else (c * 256, c * 256 + 256)
+            lo = 16 + n * HALF
+            nc.vector.tensor_tensor(
+                out=grp[(n, 0)][:, a:z, :], in0=h_sb[:, :, lo + a : lo + z].rearrange("p j t -> p t j"),
+                in1=g1n[:, 0, :].unsqueeze(1).to_broadcast([P, z - a, 4]), op=ALU.mult,
+            )
+
+        hg_ps = {}
+
+        def hg_tensor(n, tau, c, i):
+            ps = bank16(i)
+            hg_ps[(n, tau, c)] = ps
+            lo = 16 + n * HALF + c * 256 - tau
+            for j in range(4):
+                nc.tensor.matmul(ps[:, j, :], lhsT=diag[:, tau, j, :], rhs=h_sb[:, j, lo : lo + 256], start=True, stop=True)
+
+        def hg_empty(copy, n, tau, c):
+            if (n, tau) not in grp:
+                new_grp((n, tau))
+            copy(out=grp[(n, tau)][:, c * 256 : (c + 1) * 256, :], in_=hg_ps[(n, tau, c)][:].rearrange("p j t -> p t j"))
+
+        def q_hg(n, tau):
+            cs = slice(n * HALF, (n + 1) * HALF)
+            quantize(hg_c[:, tau, cs], hg_s[:, tau, cs], grp[(n, tau)][:].rearrange("p t j -> p (t j)"))
+
+        def q_weight(which, codes, scales, g):
+            quantize(codes[:, g, :], scales[:, g, :], wt[(which, g)][:].rearrange("p m j -> p (m j)"))
+
+        def mx(ps, wc, ws, xc, xs, b, lo, width, tau):
+            bs = slice(b * P, (b + 1) * P)
+            cs = slice(lo, lo + width)
+            nc.tensor.matmul_mx(
+                out=ps, lhsT=wc[:, tau, bs].bitcast(FP8X4), lhsT_scale=ws[:, tau, bs],
+                rhs=xc[:, tau, cs].bitcast(FP8X4), rhs_scale=xs[:, tau, cs], start=(tau == 0), stop=(tau == TAU - 1),
+            )
+
+        def cols(n):
+            return slice(n * HALF, (n + 1) * HALF)
+
+        s_ps = {}
+
+        def open_s(n):
+            for b in range(4):
+                s_ps[(b, n)] = bank(4 * n + b)
+
+        def stage1(n, tau):
+            for b in range(4):
+                mx(s_ps[(b, n)][:], w1_c, w1_s, hg_c, hg_s, b, n * HALF, HALF, tau)
+
+        def sig1(n):
+            for b in range(4):
+                nc.scalar.activation(out=mid[:, b, cols(n)], in_=s_ps[(b, n)][:], func=ACT.Sigmoid)
+
+        def ln1(n):
+            for b in range(4):
+                nc.scalar.activation(out=mid[:, b, cols(n)], in_=mid[:, b, cols(n)], func=ACT.Ln, bias=TINY)
+
+        def clamp(n):
+            for b in range(4):
+                nc.vector.scalar_tensor_tensor(
+                    out=mid[:, b, cols(n)], in0=s_ps[(b, n)][:], scalar=0.0, in1=mid[:, b, cols(n)], op0=ALU.min, op1=ALU.min
+                )
+
+        def ln2(n):
+            for bp in range(2):
+                sl = mid[:, 2 * bp : 2 * bp + 2, cols(n)]
+                nc.scalar.activation(out=sl, in_=sl, func=ACT.Ln, scale=-4.0, bias=TINY)
+
+        def sig2(lo, hi):
+            nc.scalar.activation(out=mid[:, :, lo:hi], in_=mid[:, :, lo:hi], func=ACT.Sigmoid, scale=-1.0)
+
+        w2_rows = []
+
+        def w2_prod(b):
+            if not w2_rows:
+                w2_rows.append(keep.tile([P, 4, TAU * F], BF16, name="w2_sb", tag="rows", align_bytes=64))
+            w2_sb = w2_rows[0]
+            nc.vector.tensor_tensor(out=w2_sb[:, b, :], in0=w2_by[:, b, :].bitcast(FP8), in1=sc_sb[:], op=ALU.mult)
+
+        def ratio(lo, hi):
+            nc.vector.scalar_tensor_tensor(
+                out=w_il[:, lo:hi, :], in0=mid[:, :, lo:hi].rearrange("p b t -> p t b"), scalar=4.0,
+                in1=v_sb[:, :, lo:hi].rearrange("p b t -> p t b"), op0=ALU.mult, op1=ALU.mult,
+            )
+
+        def eg_vector(c, tau):
+            lo, hi = CHUNKS[c]
+            new_grp(("e", c, tau))
+            nc.vector.scalar_tensor_tensor(
+                out=grp[("e", c, tau)][:, 0 : hi - lo, :], in0=w_il[:, lo + tau : hi + tau, :], scalar=1.0,
+                in1=g2_sb[:, tau, 0:4].unsqueeze(1).to_broadcast([P, hi - lo, 4]), op0=ALU.subtract, op1=ALU.mult,
+            )
+
+        g2f = keep.tile([P, TAU, 4], F32, name="g2f")
+        g2m = keep.tile([P, TAU, 4], F32, name="g2m")
+
+        def eg_scalar(c, tau):
+            lo, hi = CHUNKS[c]
+            new_grp(("e", c, tau))
+            planes = stage.tile([P, 4, 384], BF16, name="planes", bufs=2)
+            for j in range(4):
+                nc.scalar.activation(
+                    out=planes[:, j, 0 : hi - lo], in_=w_il[:, lo + tau : hi + tau, j], func=ACT.Identity,
+                    scale=g2f[:, tau, j : j + 1], bias=g2m[:, tau, j : j + 1],
+                )
+            nc.scalar.copy(out=grp[("e", c, tau)][:, 0 : hi - lo, :], in_=planes[:, :, 0 : hi - lo].rearrange("p j t -> p t j"))
+
+        PIECES = {0: ((0, 256), (256, 128)), 1: ((384, 128), (512, 256)), 2: ((768, 256),)}
+
+        def q_eg(c, tau):
+            base = CHUNKS[c][0]
+            for lo, width in PIECES[c]:
+                quantize(
+                    eg_c[:, tau, lo : lo + width], eg_s[:, tau, lo : lo + width],
+                    grp[("e", c, tau)][:, lo - base : lo - base + width, :].rearrange("p t j -> p (t j)"),
+                )
+
+        r_ps = {}
+
+        def stage2(c):
+            for lo, width in PIECES[c]:
+                n = lo // HALF
+                if lo % HALF == 0:
+                    for b in range(4):
+                        r_ps[(b, n)] = bank(4 * n + b)
+                for tau in range(TAU):
+                    for b in range(4):
+                        off = lo - n * HALF
+                        mx(r_ps[(b, n)][:, off : off + width], w2_c, w2_s, eg_c, eg_s, b, lo, width, tau)
+
+        REGIONS = {0: ((0, 384),), 1: ((384, 128), (512, 256)), 2: ((768, 256),)}
+        bias = keep.tile([P, 4], F32, name="bias")
+        out_v = out.rearrange("(p b) t -> p b t", b=4)
+        ex = {}
+
+        def exps(c):
+            for lo, width in REGIONS[c]:
+                n = lo // HALF
+                off = lo - n * HALF
+                ex[lo] = stage.tile([P, 4, 384], F32, name="ex", bufs=2)
+                for b in range(4):
+                    nc.scalar.activation(
+                        out=ex[lo][:, b, 0:width], in_=r_ps[(b, n)][:, off : off + width], func=ACT.Exp, scale=0.5, bias=bias[:, b : b + 1]
+                    )
+
+        def finish(c):
+            for lo, width in REGIONS[c]:
+                res = stage.tile([P, 4, 384], F32, name="res", bufs=2)
+                time = (lo + 512) % T
+                for bp in range(2):
+                    bs = slice(2 * bp, 2 * bp + 2)
+                    nc.vector.tensor_tensor(out=res[:, bs, 0:width], in0=ex[lo][:, bs, 0:width], in1=h_sb[:, bs, 16 + lo : 16 + lo + width], op=ALU.mult)
+                    nc.sync.dma_start(out=out_v[:, bs, time : time + width], in_=res[:, bs, 0:width])
+
+        SC, VC = nc.scalar.copy, nc.vector.tensor_copy
+        fills = [(tau, c) for tau in range(1, TAU) for c in range(2)]
+        lo_banks, hi_banks = (0, 1, 2, 3), (4, 5, 6, 7)
+
+        def hg_fill(n, i):
+            hg_tensor(n, *fills[i], hi_banks[turns[0] % 4])
+            turns[0] += 1
+
+        def hg_out(n, i):
+            hg_empty(SC, n, *fills[i])
+
+        def w1_turn(g):
+            for bp in range(2):
+                turn("w1", w1_sb[:], g, bp, hi_banks)
+                empty(SC, "w1", g, bp)
+
+        def w2_turn(g, copy):
+            for bp in range(2):
+                turn("w2", w2_rows[0][:], g, bp, lo_banks)
+                empty(copy, "w2", g, bp)
+
+        hg_vector(0)
+        for i in range(6):
+            hg_fill(0, i)
+            hg_out(0, i)
+        for tau in range(TAU):
+            q_hg(0, tau)
+        open_s(0)
+        for g in range(TAU):
+            w1_turn(g)
+        q_weight("w1", w1_c, w1_s, 0)
+        hg_vector(1, 0)
+        q_weight("w1", w1_c, w1_s, 1)
+        q_weight("w1", w1_c, w1_s, 2)
+        q_weight("w1", w1_c, w1_s, 3)
+        hg_vector(1, 1)
+        stage1(0, 0)
+        for i in range(2):
+            hg_fill(1, i)
+            hg_out(1, i)
+        stage1(0, 1)
+        stage1(0, 2)
+        stage1(0, 3)
+        sig1(0)
+        for i in range(2, 6):
+            hg_fill(1, i)
+            hg_out(1, i)
+        q_hg(1, 0)
+        w2_prod(0)
+        q_hg(1, 1)
+        w2_prod(1)
+        q_hg(1, 2)
+        q_hg(1, 3)
+        open_s(1)
+        for tau in range(TAU):
+            stage1(1, tau)
+        ln1(0)
+        w2_prod(2)
+        clamp(0)
+        ln2(0)
+        w2_prod(3)
+        nc.vector.tensor_scalar(out=bias[:], in0=mu_sb[:, 0:4], scalar1=-0.5, scalar2=None, op0=ALU.mult)
+        nc.vector.tensor_copy(out=g2f[:], in_=g2_sb[:, :, 0:4])
+        sig2(0, HALF)
+        sig1(1)
+        turns[0] = 0
+        w2_turn(0, VC)
+        nc.vector.tensor_scalar(out=g2m[:], in0=g2f[:], scalar1=-1.0, scalar2=None, op0=ALU.mult)
+        ratio(0, HALF)
+        ln1(1)
+        q_weight("w2", w2_c, w2_s, 0)
+        eg_vector(0, 0)
+        eg_vector(0, 1)
+        q_eg(0, 0)
+        w2_turn(1, SC)
+        clamp(1)
+        ln2(1)
+        eg_vector(0, 2)
+        q_eg(0, 1)
+        q_weight("w2", w2_c, w2_s, 1)
+        eg_vector(0, 3)
+        q_eg(0, 2)
+        sig2(HALF, T)
+        w2_turn(2, SC)
+        w2_turn(3, SC)
+        q_eg(0, 3)
+        ratio(HALF, T)
+        nc.vector.tensor_copy(out=w_il[:, T : T + 3, :], in_=w_il[:, 0:3, :])
+        eg_scalar(1, 3)
+        eg_vector(1, 0)
+        q_weight("w2", w2_c, w2_s, 2)
+        q_weight("w2", w2_c, w2_s, 3)
+        stage2(0)
+        eg_vector(1, 1)
+        q_eg(1, 0)
+        eg_scalar(1, 2)
+        eg_vector(2, 0)
+        q_eg(1, 1)
+        exps(0)
+        eg_scalar(2, 3)
+        eg_vector(2, 1)
+        q_eg(2, 0)
+        q_eg(1, 3)
+        q_eg(1, 2)
+        stage2(1)
+        eg_vector(2, 2)
+        q_eg(2, 1)
+        exps(1)
+        finish(0)
+        q_eg(2, 2)
+        q_eg(2, 3)
+        stage2(2)
+        finish(1)
+        exps(2)
+        finish(2)

@@ -49,10 +49,9 @@ def tile_convolutivenmfexponentiatedupdate_kernel(tc, v, h, w1, g1, w2_bytes, w2
         w2_v = w2_bytes.rearrange("(m b) k -> m b k", b=4)
         nc.scalar.dma_start(out=g1_sb[:, :, 0:4], in_=g1.rearrange("(a p j) -> p a j", a=TAU, j=4))
         nc.sync.dma_start(out=h_sb[:, :, 12:528], in_=h_v[:, :, 508:T])
-        for g in range(TAU):
-            nc.sync.dma_start(out=w1_sb[:, :, g * 512 : (g + 1) * 512], in_=w1_v[:, :, g * 512 : (g + 1) * 512])
-            if g == 1:
-                nc.sync.dma_start(out=h_sb[:, :, 528:1040], in_=h_v[:, :, 0:512])
+        for b in range(0, 4, 2):
+            nc.sync.dma_start(out=w1_sb[:, b : b + 2, :], in_=w1_v[:, b : b + 2, :])
+        nc.sync.dma_start(out=h_sb[:, :, 528:1040], in_=h_v[:, :, 0:512])
         for b in range(0, 4, 2):
             nc.sync.dma_start(out=w2_by[:, b : b + 2, :], in_=w2_v[:, b : b + 2, :])
         nc.sync.dma_start(out=sc_sb[:], in_=w2_scale.rearrange("o k -> (o k)").partition_broadcast(P))
@@ -106,7 +105,7 @@ def tile_convolutivenmfexponentiatedupdate_kernel(tc, v, h, w1, g1, w2_bytes, w2
 
         def empty(copy, which, g, bp):
             if (which, g) not in wt:
-                wt[(which, g)] = stage.tile([P, 512, 4], BF16, name="wt", align_bytes=64)
+                wt[(which, g)] = stage.tile([P, 512, 4], BF16, name="wt", align_bytes=64, bufs=4)
             dst = wt[(which, g)][:, bp * 256 : (bp + 1) * 256, :].rearrange("p m j -> p (m j)").bitcast(F32)
             copy(
                 out=dst.rearrange("p (b m u) -> p b m u", b=2, u=2),
@@ -118,14 +117,15 @@ def tile_convolutivenmfexponentiatedupdate_kernel(tc, v, h, w1, g1, w2_bytes, w2
         def new_grp(key):
             grp[key] = stage.tile([P, HALF, 4], BF16, name="grouped", align_bytes=64, bufs=8)
 
-        def hg_vector(n, c=None):
+        def hg_vector(n, c):
             if (n, 0) not in grp:
                 new_grp((n, 0))
-            a, z = (0, HALF) if c is None else (c * 256, c * 256 + 256)
+            a, z = c * 256, c * 256 + 256
             lo = 16 + n * HALF
             nc.vector.tensor_tensor(
-                out=grp[(n, 0)][:, a:z, :], in0=h_sb[:, :, lo + a : lo + z].rearrange("p j t -> p t j"),
-                in1=g1n[:, 0, :].unsqueeze(1).to_broadcast([P, z - a, 4]), op=ALU.mult,
+                out=grp[(n, 0)][:, a:z, :].rearrange("p (c i) j -> p c j i", i=8),
+                in0=h_sb[:, :, lo + a : lo + z].rearrange("p j (c i) -> p c j i", i=8),
+                in1=g1n[:, 0, :].unsqueeze(1).unsqueeze(3).to_broadcast([P, 32, 4, 8]), op=ALU.mult,
             )
 
         hg_ps = {}
@@ -146,8 +146,9 @@ def tile_convolutivenmfexponentiatedupdate_kernel(tc, v, h, w1, g1, w2_bytes, w2
             cs = slice(n * HALF, (n + 1) * HALF)
             quantize(hg_c[:, tau, cs], hg_s[:, tau, cs], grp[(n, tau)][:].rearrange("p t j -> p (t j)"))
 
-        def q_weight(which, codes, scales, g):
-            quantize(codes[:, g, :], scales[:, g, :], wt[(which, g)][:].rearrange("p m j -> p (m j)"))
+        def q_weight(which, codes, scales, g, bp):
+            ms = slice(bp * 256, (bp + 1) * 256)
+            quantize(codes[:, g, ms], scales[:, g, ms], wt[(which, g)][:, ms, :].rearrange("p m j -> p (m j)"))
 
         def mx(ps, wc, ws, xc, xs, b, lo, width, tau):
             bs = slice(b * P, (b + 1) * P)
@@ -166,28 +167,27 @@ def tile_convolutivenmfexponentiatedupdate_kernel(tc, v, h, w1, g1, w2_bytes, w2
             for b in range(4):
                 s_ps[(b, n)] = bank(4 * n + b)
 
-        def stage1(n, tau):
-            for b in range(4):
+        def stage1(n, tau, bp):
+            for b in range(2 * bp, 2 * bp + 2):
                 mx(s_ps[(b, n)][:], w1_c, w1_s, hg_c, hg_s, b, n * HALF, HALF, tau)
 
-        def sig1(n):
-            for b in range(4):
+        def sig1(n, bp):
+            for b in range(2 * bp, 2 * bp + 2):
                 nc.scalar.activation(out=mid[:, b, cols(n)], in_=s_ps[(b, n)][:], func=ACT.Sigmoid)
 
-        def ln1(n):
-            for b in range(4):
+        def ln1(n, bp):
+            for b in range(2 * bp, 2 * bp + 2):
                 nc.scalar.activation(out=mid[:, b, cols(n)], in_=mid[:, b, cols(n)], func=ACT.Ln, bias=TINY)
 
-        def clamp(n):
-            for b in range(4):
+        def clamp(n, bp):
+            for b in range(2 * bp, 2 * bp + 2):
                 nc.vector.scalar_tensor_tensor(
                     out=mid[:, b, cols(n)], in0=s_ps[(b, n)][:], scalar=0.0, in1=mid[:, b, cols(n)], op0=ALU.min, op1=ALU.min
                 )
 
-        def ln2(n):
-            for bp in range(2):
-                sl = mid[:, 2 * bp : 2 * bp + 2, cols(n)]
-                nc.scalar.activation(out=sl, in_=sl, func=ACT.Ln, scale=-4.0, bias=TINY)
+        def ln2(n, bp):
+            sl = mid[:, 2 * bp : 2 * bp + 2, cols(n)]
+            nc.scalar.activation(out=sl, in_=sl, func=ACT.Ln, scale=-4.0, bias=TINY)
 
         def sig2(lo, hi):
             nc.scalar.activation(out=mid[:, :, lo:hi], in_=mid[:, :, lo:hi], func=ACT.Sigmoid, scale=-1.0)
@@ -201,19 +201,21 @@ def tile_convolutivenmfexponentiatedupdate_kernel(tc, v, h, w1, g1, w2_bytes, w2
             nc.vector.tensor_tensor(out=w2_sb[:, b, :], in0=w2_by[:, b, :].bitcast(FP8), in1=sc_sb[:], op=ALU.mult)
 
         def ratio(lo, hi):
-            nc.vector.scalar_tensor_tensor(
-                out=w_il[:, lo:hi, :], in0=mid[:, :, lo:hi].rearrange("p b t -> p t b"), scalar=4.0,
-                in1=v_sb[:, :, lo:hi].rearrange("p b t -> p t b"), op0=ALU.mult, op1=ALU.mult,
+            nc.vector.tensor_tensor(
+                out=w_il[:, lo:hi, :].rearrange("p (c i) b -> p c b i", i=4),
+                in0=mid[:, :, lo:hi].rearrange("p b (c i) -> p c b i", i=4),
+                in1=v_sb[:, :, lo:hi].rearrange("p b (c i) -> p c b i", i=4), op=ALU.mult,
             )
 
         def eg_vector(c, tau):
             lo, hi = CHUNKS[c]
             new_grp(("e", c, tau))
             nc.vector.scalar_tensor_tensor(
-                out=grp[("e", c, tau)][:, 0 : hi - lo, :], in0=w_il[:, lo + tau : hi + tau, :], scalar=1.0,
-                in1=g2_sb[:, tau, 0:4].unsqueeze(1).to_broadcast([P, hi - lo, 4]), op0=ALU.subtract, op1=ALU.mult,
+                out=grp[("e", c, tau)][:, 0 : hi - lo, :], in0=w_il[:, lo + tau : hi + tau, :], scalar=0.25,
+                in1=g2x4[:, tau, :].unsqueeze(1).to_broadcast([P, hi - lo, 4]), op0=ALU.subtract, op1=ALU.mult,
             )
 
+        g2x4 = keep.tile([P, TAU, 4], BF16, name="g2x4")
         g2f = keep.tile([P, TAU, 4], F32, name="g2f")
         g2m = keep.tile([P, TAU, 4], F32, name="g2m")
 
@@ -226,7 +228,10 @@ def tile_convolutivenmfexponentiatedupdate_kernel(tc, v, h, w1, g1, w2_bytes, w2
                     out=planes[:, j, 0 : hi - lo], in_=w_il[:, lo + tau : hi + tau, j], func=ACT.Identity,
                     scale=g2f[:, tau, j : j + 1], bias=g2m[:, tau, j : j + 1],
                 )
-            nc.scalar.copy(out=grp[("e", c, tau)][:, 0 : hi - lo, :], in_=planes[:, :, 0 : hi - lo].rearrange("p j t -> p t j"))
+            nc.scalar.copy(
+                out=grp[("e", c, tau)][:, 0 : hi - lo, :].rearrange("p (c i) j -> p c j i", i=8),
+                in_=planes[:, :, 0 : hi - lo].rearrange("p j (c i) -> p c j i", i=8),
+            )
 
         PIECES = {0: ((0, 256), (256, 128)), 1: ((384, 128), (512, 256)), 2: ((768, 256),)}
 
@@ -268,12 +273,12 @@ def tile_convolutivenmfexponentiatedupdate_kernel(tc, v, h, w1, g1, w2_bytes, w2
 
         def finish(c):
             for lo, width in REGIONS[c]:
-                res = stage.tile([P, 4, 384], F32, name="res", bufs=2)
                 time = (lo + 512) % T
                 for bp in range(2):
                     bs = slice(2 * bp, 2 * bp + 2)
-                    nc.vector.tensor_tensor(out=res[:, bs, 0:width], in0=ex[lo][:, bs, 0:width], in1=h_sb[:, bs, 16 + lo : 16 + lo + width], op=ALU.mult)
-                    nc.sync.dma_start(out=out_v[:, bs, time : time + width], in_=res[:, bs, 0:width])
+                    res = stage.tile([P, 2, 384], F32, name="res", bufs=6)
+                    nc.vector.tensor_tensor(out=res[:, :, 0:width], in0=ex[lo][:, bs, 0:width], in1=h_sb[:, bs, 16 + lo : 16 + lo + width], op=ALU.mult)
+                    nc.sync.dma_start(out=out_v[:, bs, time : time + width], in_=res[:, :, 0:width])
 
         SC, VC = nc.scalar.copy, nc.vector.tensor_copy
         fills = [(tau, c) for tau in range(1, TAU) for c in range(2)]
@@ -286,17 +291,22 @@ def tile_convolutivenmfexponentiatedupdate_kernel(tc, v, h, w1, g1, w2_bytes, w2
         def hg_out(n, i):
             hg_empty(SC, n, *fills[i])
 
-        def w1_turn(g):
-            for bp in range(2):
-                turn("w1", w1_sb[:], g, bp, hi_banks)
-                empty(SC, "w1", g, bp)
+        def w1_turn(bp, g):
+            turn("w1", w1_sb[:], g, bp, hi_banks)
+            empty(SC, "w1", g, bp)
 
-        def w2_turn(g, copy):
-            for bp in range(2):
-                turn("w2", w2_rows[0][:], g, bp, lo_banks)
-                empty(copy, "w2", g, bp)
+        def w2_turn(bp, g, copy):
+            turn("w2", w2_rows[0][:], g, bp, lo_banks)
+            empty(copy, "w2", g, bp)
 
-        hg_vector(0)
+        def q1(g, bp):
+            q_weight("w1", w1_c, w1_s, g, bp)
+
+        def q2(g, bp):
+            q_weight("w2", w2_c, w2_s, g, bp)
+
+        hg_vector(0, 0)
+        hg_vector(0, 1)
         for i in range(6):
             hg_fill(0, i)
             hg_out(0, i)
@@ -304,69 +314,85 @@ def tile_convolutivenmfexponentiatedupdate_kernel(tc, v, h, w1, g1, w2_bytes, w2
             q_hg(0, tau)
         open_s(0)
         for g in range(TAU):
-            w1_turn(g)
-        q_weight("w1", w1_c, w1_s, 0)
+            w1_turn(0, g)
+        for g in range(TAU):
+            q1(g, 0)
+        for g in range(TAU):
+            w1_turn(1, g)
+        for tau in range(TAU):
+            stage1(0, tau, 0)
         hg_vector(1, 0)
-        q_weight("w1", w1_c, w1_s, 1)
-        q_weight("w1", w1_c, w1_s, 2)
-        q_weight("w1", w1_c, w1_s, 3)
+        for g in range(TAU):
+            q1(g, 1)
+        for tau in range(TAU):
+            stage1(0, tau, 1)
         hg_vector(1, 1)
-        stage1(0, 0)
-        for i in range(2):
+        sig1(0, 0)
+        sig1(0, 1)
+        for i in range(6):
             hg_fill(1, i)
+        for i in range(3):
             hg_out(1, i)
-        stage1(0, 1)
-        stage1(0, 2)
-        stage1(0, 3)
-        sig1(0)
-        for i in range(2, 6):
-            hg_fill(1, i)
+        ln1(0, 0)
+        ln1(0, 1)
+        for i in range(3, 6):
             hg_out(1, i)
         q_hg(1, 0)
         w2_prod(0)
         q_hg(1, 1)
         w2_prod(1)
+        w2_prod(2)
+        clamp(0, 0)
+        clamp(0, 1)
         q_hg(1, 2)
         q_hg(1, 3)
         open_s(1)
         for tau in range(TAU):
-            stage1(1, tau)
-        ln1(0)
-        w2_prod(2)
-        clamp(0)
-        ln2(0)
+            stage1(1, tau, 0)
+            stage1(1, tau, 1)
+        ln2(0, 0)
+        ln2(0, 1)
         w2_prod(3)
         nc.vector.tensor_scalar(out=bias[:], in0=mu_sb[:, 0:4], scalar1=-0.5, scalar2=None, op0=ALU.mult)
-        nc.vector.tensor_copy(out=g2f[:], in_=g2_sb[:, :, 0:4])
+        nc.vector.tensor_scalar(out=g2x4[:], in0=g2_sb[:, :, 0:4], scalar1=4.0, scalar2=None, op0=ALU.mult)
+        nc.vector.tensor_copy(out=g2f[:], in_=g2x4[:])
         sig2(0, HALF)
-        sig1(1)
+        sig1(1, 0)
+        sig1(1, 1)
         turns[0] = 0
-        w2_turn(0, VC)
-        nc.vector.tensor_scalar(out=g2m[:], in0=g2f[:], scalar1=-1.0, scalar2=None, op0=ALU.mult)
+        for g in range(2):
+            w2_turn(0, g, VC)
+        nc.vector.tensor_scalar(out=g2m[:], in0=g2_sb[:, :, 0:4], scalar1=-1.0, scalar2=None, op0=ALU.mult)
         ratio(0, HALF)
-        ln1(1)
-        q_weight("w2", w2_c, w2_s, 0)
+        ln1(1, 0)
+        ln1(1, 1)
+        q2(0, 0)
+        q2(1, 0)
         eg_vector(0, 0)
         eg_vector(0, 1)
         q_eg(0, 0)
-        w2_turn(1, SC)
-        clamp(1)
-        ln2(1)
+        for g in range(2, 4):
+            w2_turn(0, g, SC)
+        clamp(1, 0)
+        clamp(1, 1)
+        ln2(1, 0)
+        ln2(1, 1)
         eg_vector(0, 2)
         q_eg(0, 1)
-        q_weight("w2", w2_c, w2_s, 1)
+        q2(2, 0)
+        q2(3, 0)
         eg_vector(0, 3)
         q_eg(0, 2)
         sig2(HALF, T)
-        w2_turn(2, SC)
-        w2_turn(3, SC)
+        for g in range(TAU):
+            w2_turn(1, g, SC)
         q_eg(0, 3)
         ratio(HALF, T)
         nc.vector.tensor_copy(out=w_il[:, T : T + 3, :], in_=w_il[:, 0:3, :])
         eg_scalar(1, 3)
         eg_vector(1, 0)
-        q_weight("w2", w2_c, w2_s, 2)
-        q_weight("w2", w2_c, w2_s, 3)
+        for g in range(TAU):
+            q2(g, 1)
         stage2(0)
         eg_vector(1, 1)
         q_eg(1, 0)

@@ -18,7 +18,8 @@ FLOPS = 2 * 2 * F * TAU * K * T
 
 HALF = 512
 TINY = 2.0 ** -60
-CHUNKS = ((0, 384), (384, 768), (768, T))
+CHUNKS = ((0, 512), (512, 768), (768, T))
+SIG2 = ((0, 576), (576, T))
 
 
 def tile_convolutivenmfexponentiatedupdate_kernel(tc, v, h, w1, g1, w2_bytes, w2_scale, g2, mu, out):
@@ -26,14 +27,11 @@ def tile_convolutivenmfexponentiatedupdate_kernel(tc, v, h, w1, g1, w2_bytes, w2
     with ExitStack() as ctx:
         ctx.enter_context(tc.manual_schedule())
         keep = ctx.enter_context(tc.tile_pool(name="keep", bufs=1))
-        stage = ctx.enter_context(tc.tile_pool(name="stage", bufs=3))
+        stage = ctx.enter_context(tc.tile_pool(name="stage", bufs=1))
         psum = ctx.enter_context(tc.psum_pool(name="psum", bufs=1))
 
         def bank(i):
             return psum.tile([P, 512], F32, name="bank%d" % i, tag="bank%d" % i)
-
-        def bank16(i):
-            return psum.tile([P, 4, 256], BF16, name="bank%d" % i, tag="bank%d" % i)
 
         h_sb = keep.tile([P, 4, 16 + T], BF16, name="h_sb", align_bytes=64)
         w1_sb = keep.tile([P, 4, TAU * K], BF16, name="w1_sb", tag="rows", align_bytes=64)
@@ -43,6 +41,8 @@ def tile_convolutivenmfexponentiatedupdate_kernel(tc, v, h, w1, g1, w2_bytes, w2
         g1_sb = keep.tile([P, TAU, 16], BF16, name="g1_sb")
         g2_sb = keep.tile([P, TAU, 16], BF16, name="g2_sb")
         mu_sb = keep.tile([P, 16], BF16, name="mu_sb")
+        wz = keep.tile([P, 256], F32, name="wz")
+        nc.gpsimd.memset(wz[:], 0.0)
         h_v = h.rearrange("(p j) t -> p j t", j=4)
         v_v = v.rearrange("(p j) t -> p j t", j=4)
         w1_v = w1.rearrange("(m b) k -> m b k", b=4)
@@ -60,21 +60,17 @@ def tile_convolutivenmfexponentiatedupdate_kernel(tc, v, h, w1, g1, w2_bytes, w2
         nc.scalar.dma_start(out=g2_sb[:, :, 0:4], in_=g2.rearrange("(a p j) -> p a j", a=TAU, j=4))
         nc.scalar.dma_start(out=mu_sb[:, 0:4], in_=mu.rearrange("(p j) -> p j", j=4))
 
-        ident16 = keep.tile([P, P], BF16, name="ident16")
-        make_identity(nc, ident16[:])
         ident = keep.tile([P, P], F32, name="ident")
         make_identity(nc, ident[:])
+        ident16 = keep.tile([P, P], BF16, name="ident16")
+        make_identity(nc, ident16[:])
         dummy = keep.tile([P, 2], F32, name="dummy")
         nc.vector.memset(dummy[:], 0.0)
         nc.scalar.activation(out=dummy[:, 1:2], in_=dummy[:, 0:1], func=ACT.Sigmoid)
 
         g1n = keep.tile([P, TAU, 4], BF16, name="g1n")
         nc.vector.tensor_scalar(out=g1n[:], in0=g1_sb[:, :, 0:4], scalar1=-1.0, scalar2=None, op0=ALU.mult)
-        diag = keep.tile([P, TAU, 4, P], BF16, name="diag")
-        for tau in range(1, TAU):
-            for j in range(4):
-                nc.vector.tensor_scalar(out=diag[:, tau, j, :], in0=ident16[:], scalar1=g1n[:, tau, j : j + 1], scalar2=None, op0=ALU.mult)
-
+        h_il = keep.tile([P, 16 + T, 4], BF16, name="h_il", align_bytes=64)
         hg_c = keep.tile([P, TAU, T], U32, name="hg_c", align_bytes=64)
         hg_s = keep.tile([P, TAU, T], U8, name="hg_s", align_bytes=64)
         eg_c = keep.tile([P, TAU, T], U32, name="eg_c", align_bytes=64)
@@ -84,19 +80,40 @@ def tile_convolutivenmfexponentiatedupdate_kernel(tc, v, h, w1, g1, w2_bytes, w2
         w2_c = keep.tile([P, TAU, 512], U32, name="w2_c", align_bytes=64)
         w2_s = keep.tile([P, TAU, 512], U8, name="w2_s", align_bytes=64)
         mid = keep.tile([P, 4, T], F32, name="mid", align_bytes=64)
-        w_il = keep.tile([P, T + 3, 4], F32, name="w_il", align_bytes=64)
+        ratio_sb = keep.tile([P, 4, T + 16], F32, name="ratio_sb", align_bytes=64)
+
+
+        chunks = len(CHUNKS)
+
+        def tagged(shape, dt, name, slot):
+            return stage.tile(shape, dt, name="%s%d" % (name, slot), tag="%s%d" % (name, slot), align_bytes=64)
 
         def quantize(codes, scales, grouped):
             nc.vector.quantize_mx(out=codes.bitcast(FP8X4), scales=scales, in_=grouped)
 
-        wt = {}
-        turned = {}
-        turns = [4]
+        def cols(n):
+            return slice(n * HALF, (n + 1) * HALF)
 
-        def turn(which, src, g, bp, banks):
-            ps = bank(banks[turns[0] % 4])
-            turns[0] += 1
-            turned[(which, g, bp)] = ps
+        HI = ((12, 272), (272, 528), (528, 784), (784, 1040))
+
+        def hiv(k):
+            lo, hi = HI[k]
+            nc.vector.tensor_copy(out=h_il[:, lo:hi, :], in_=h_sb[:, :, lo:hi].rearrange("p j t -> p t j"))
+
+        def his(k):
+            lo, hi = HI[k]
+            nc.scalar.copy(out=h_il[:, lo:hi, :], in_=h_sb[:, :, lo:hi].rearrange("p j t -> p t j"))
+
+        wp = psum.tile([P, 512], F32, name="warm", tag="bank0")
+
+        def warm(k):
+            nc.tensor.matmul(wp[:, 0:256], lhsT=ident[:], rhs=wz[:], start=True, stop=True)
+
+        tiles = {}
+
+        def turn(which, src, g, bp, i):
+            ps = bank(i)
+            tiles[("ps", which, g, bp)] = ps
             words = src.bitcast(F32)
             for b2 in range(2):
                 for u in range(2):
@@ -104,51 +121,64 @@ def tile_convolutivenmfexponentiatedupdate_kernel(tc, v, h, w1, g1, w2_bytes, w2
                     nc.tensor.transpose(ps[:, col : col + P], words[:, bp * 2 + b2, 256 * g + u : 256 * (g + 1) : 2], ident[:])
 
         def empty(copy, which, g, bp):
-            if (which, g) not in wt:
-                wt[(which, g)] = stage.tile([P, 512, 4], BF16, name="wt", align_bytes=64, bufs=4)
-            dst = wt[(which, g)][:, bp * 256 : (bp + 1) * 256, :].rearrange("p m j -> p (m j)").bitcast(F32)
+            if ("wt", which, g) not in tiles:
+                tiles[("wt", which, g)] = tagged([P, 512, 4], BF16, "wt", g)
+            dst = tiles[("wt", which, g)][:, bp * 256 : (bp + 1) * 256, :].rearrange("p m j -> p (m j)").bitcast(F32)
             copy(
                 out=dst.rearrange("p (b m u) -> p b m u", b=2, u=2),
-                in_=turned[(which, g, bp)][:].rearrange("p (b u m) -> p b m u", b=2, u=2),
+                in_=tiles[("ps", which, g, bp)][:].rearrange("p (b u m) -> p b m u", b=2, u=2),
             )
 
-        grp = {}
+        def w1t(g, bp):
+            turn("w1", w1_sb[:], g, bp, 4 + g)
 
-        def new_grp(key):
-            grp[key] = stage.tile([P, HALF, 4], BF16, name="grouped", align_bytes=64, bufs=8)
+        def w1c(g, bp):
+            empty(nc.scalar.copy, "w1", g, bp)
 
-        def hg_vector(n, c):
-            if (n, 0) not in grp:
-                new_grp((n, 0))
-            a, z = c * 256, c * 256 + 256
-            lo = 16 + n * HALF
-            nc.vector.tensor_tensor(
-                out=grp[(n, 0)][:, a:z, :].rearrange("p (c i) j -> p c j i", i=8),
-                in0=h_sb[:, :, lo + a : lo + z].rearrange("p j (c i) -> p c j i", i=8),
-                in1=g1n[:, 0, :].unsqueeze(1).unsqueeze(3).to_broadcast([P, 32, 4, 8]), op=ALU.mult,
-            )
+        def w1v(g, bp):
+            empty(nc.vector.tensor_copy, "w1", g, bp)
 
-        hg_ps = {}
+        def w2t(g, bp):
+            turn("w2", tiles["w2"][:], g, bp, g)
 
-        def hg_tensor(n, tau, c, i):
-            ps = bank16(i)
-            hg_ps[(n, tau, c)] = ps
-            lo = 16 + n * HALF + c * 256 - tau
-            for j in range(4):
-                nc.tensor.matmul(ps[:, j, :], lhsT=diag[:, tau, j, :], rhs=h_sb[:, j, lo : lo + 256], start=True, stop=True)
+        def w2c(g, bp):
+            empty(nc.scalar.copy, "w2", g, bp)
 
-        def hg_empty(copy, n, tau, c):
-            if (n, tau) not in grp:
-                new_grp((n, tau))
-            copy(out=grp[(n, tau)][:, c * 256 : (c + 1) * 256, :], in_=hg_ps[(n, tau, c)][:].rearrange("p j t -> p t j"))
-
-        def q_hg(n, tau):
-            cs = slice(n * HALF, (n + 1) * HALF)
-            quantize(hg_c[:, tau, cs], hg_s[:, tau, cs], grp[(n, tau)][:].rearrange("p t j -> p (t j)"))
+        def w2v(g, bp):
+            empty(nc.vector.tensor_copy, "w2", g, bp)
 
         def q_weight(which, codes, scales, g, bp):
             ms = slice(bp * 256, (bp + 1) * 256)
-            quantize(codes[:, g, ms], scales[:, g, ms], wt[(which, g)][:, ms, :].rearrange("p m j -> p (m j)"))
+            quantize(codes[:, g, ms], scales[:, g, ms], tiles[("wt", which, g)][:, ms, :].rearrange("p m j -> p (m j)"))
+
+        def q1(g, bp):
+            q_weight("w1", w1_c, w1_s, g, bp)
+
+        def q2(g, bp):
+            q_weight("w2", w2_c, w2_s, g, bp)
+
+        def hgm(n, tau):
+            tiles[("hg", n, tau)] = tagged([P, HALF, 4], BF16, "grp", (n * TAU + tau) % 6)
+            lo = 16 + n * HALF - tau
+            nc.vector.tensor_tensor(
+                out=tiles[("hg", n, tau)][:], in0=h_il[:, lo : lo + HALF, :],
+                in1=g1n[:, tau, :].unsqueeze(1).to_broadcast([P, HALF, 4]), op=ALU.mult,
+            )
+
+        g1f = keep.tile([P, TAU, 4], F32, name="g1f")
+
+        def hgp(n, tau):
+            tiles[("hp", n, tau)] = tagged([P, 4, 512], BF16, "pl", 3)
+            lo = 16 + n * HALF - tau
+            for j in range(4):
+                nc.scalar.activation(out=tiles[("hp", n, tau)][:, j, :], in_=h_sb[:, j, lo : lo + HALF], func=ACT.Copy, scale=g1f[:, tau, j : j + 1])
+
+        def hgi(n, tau):
+            tiles[("hg", n, tau)] = tagged([P, HALF, 4], BF16, "grp", (n * TAU + tau) % 6)
+            nc.scalar.copy(out=tiles[("hg", n, tau)][:], in_=tiles[("hp", n, tau)][:].rearrange("p j t -> p t j"))
+
+        def qh(n, tau):
+            quantize(hg_c[:, tau, cols(n)], hg_s[:, tau, cols(n)], tiles[("hg", n, tau)][:].rearrange("p t j -> p (t j)"))
 
         def mx(ps, wc, ws, xc, xs, b, lo, width, tau):
             bs = slice(b * P, (b + 1) * P)
@@ -158,261 +188,377 @@ def tile_convolutivenmfexponentiatedupdate_kernel(tc, v, h, w1, g1, w2_bytes, w2
                 rhs=xc[:, tau, cs].bitcast(FP8X4), rhs_scale=xs[:, tau, cs], start=(tau == 0), stop=(tau == TAU - 1),
             )
 
-        def cols(n):
-            return slice(n * HALF, (n + 1) * HALF)
-
-        s_ps = {}
-
-        def open_s(n):
-            for b in range(4):
-                s_ps[(b, n)] = bank(4 * n + b)
-
-        def stage1(n, tau, bp):
+        def st1(n, tau, bp):
             for b in range(2 * bp, 2 * bp + 2):
-                mx(s_ps[(b, n)][:], w1_c, w1_s, hg_c, hg_s, b, n * HALF, HALF, tau)
+                if tau == 0:
+                    tiles[("s", b, n)] = bank(4 * n + b)
+                mx(tiles[("s", b, n)][:], w1_c, w1_s, hg_c, hg_s, b, n * HALF, HALF, tau)
 
-        def sig1(n, bp):
-            for b in range(2 * bp, 2 * bp + 2):
-                nc.scalar.activation(out=mid[:, b, cols(n)], in_=s_ps[(b, n)][:], func=ACT.Sigmoid)
+        def sig1(n, b):
+            nc.scalar.activation(out=mid[:, b, cols(n)], in_=tiles[("s", b, n)][:], func=ACT.Sigmoid)
 
         def ln1(n, bp):
-            for b in range(2 * bp, 2 * bp + 2):
-                nc.scalar.activation(out=mid[:, b, cols(n)], in_=mid[:, b, cols(n)], func=ACT.Ln, bias=TINY)
+            sl = mid[:, 2 * bp : 2 * bp + 2, cols(n)]
+            nc.scalar.activation(out=sl, in_=sl, func=ACT.Ln, bias=TINY)
 
-        def clamp(n, bp):
-            for b in range(2 * bp, 2 * bp + 2):
-                nc.vector.scalar_tensor_tensor(
-                    out=mid[:, b, cols(n)], in0=s_ps[(b, n)][:], scalar=0.0, in1=mid[:, b, cols(n)], op0=ALU.min, op1=ALU.min
-                )
+        def clamp(n, b):
+            nc.vector.scalar_tensor_tensor(
+                out=mid[:, b, cols(n)], in0=tiles[("s", b, n)][:], scalar=0.0, in1=mid[:, b, cols(n)], op0=ALU.min, op1=ALU.min
+            )
 
         def ln2(n, bp):
             sl = mid[:, 2 * bp : 2 * bp + 2, cols(n)]
             nc.scalar.activation(out=sl, in_=sl, func=ACT.Ln, scale=-4.0, bias=TINY)
 
-        def sig2(lo, hi):
+        def sig2(k):
+            lo, hi = SIG2[k]
             nc.scalar.activation(out=mid[:, :, lo:hi], in_=mid[:, :, lo:hi], func=ACT.Sigmoid, scale=-1.0)
 
-        w2_rows = []
+        def prod(b):
+            if "w2" not in tiles:
+                tiles["w2"] = keep.tile([P, 4, TAU * F], BF16, name="w2_sb", tag="rows", align_bytes=64)
+            nc.vector.tensor_tensor(out=tiles["w2"][:, b, :], in0=w2_by[:, b, :].bitcast(FP8), in1=sc_sb[:], op=ALU.mult)
 
-        def w2_prod(b):
-            if not w2_rows:
-                w2_rows.append(keep.tile([P, 4, TAU * F], BF16, name="w2_sb", tag="rows", align_bytes=64))
-            w2_sb = w2_rows[0]
-            nc.vector.tensor_tensor(out=w2_sb[:, b, :], in0=w2_by[:, b, :].bitcast(FP8), in1=sc_sb[:], op=ALU.mult)
+        def rat(k):
+            lo, hi = SIG2[k]
+            nc.vector.tensor_tensor(out=ratio_sb[:, :, lo:hi], in0=mid[:, :, lo:hi], in1=v_sb[:, :, lo:hi], op=ALU.mult)
 
-        def ratio(lo, hi):
-            nc.vector.tensor_tensor(
-                out=w_il[:, lo:hi, :].rearrange("p (c i) b -> p c b i", i=4),
-                in0=mid[:, :, lo:hi].rearrange("p b (c i) -> p c b i", i=4),
-                in1=v_sb[:, :, lo:hi].rearrange("p b (c i) -> p c b i", i=4), op=ALU.mult,
-            )
+        def wrap():
+            nc.vector.tensor_copy(out=ratio_sb[:, :, T : T + 3], in_=ratio_sb[:, :, 0:3])
 
-        def eg_vector(c, tau):
-            lo, hi = CHUNKS[c]
-            new_grp(("e", c, tau))
-            nc.vector.scalar_tensor_tensor(
-                out=grp[("e", c, tau)][:, 0 : hi - lo, :], in0=w_il[:, lo + tau : hi + tau, :], scalar=0.25,
-                in1=g2x4[:, tau, :].unsqueeze(1).to_broadcast([P, hi - lo, 4]), op0=ALU.subtract, op1=ALU.mult,
-            )
-
-        g2x4 = keep.tile([P, TAU, 4], BF16, name="g2x4")
         g2f = keep.tile([P, TAU, 4], F32, name="g2f")
         g2m = keep.tile([P, TAU, 4], F32, name="g2m")
+        g2x4 = keep.tile([P, TAU, 4], F32, name="g2x4")
+        bias = keep.tile([P, 4], F32, name="bias")
 
-        def eg_scalar(c, tau):
+        def consts():
+            nc.vector.tensor_scalar(out=bias[:], in0=mu_sb[:, 0:4], scalar1=-0.5, scalar2=None, op0=ALU.mult)
+            nc.vector.tensor_copy(out=g2f[:], in_=g2_sb[:, :, 0:4])
+            nc.vector.tensor_scalar(out=g2m[:], in0=g2_sb[:, :, 0:4], scalar1=-1.0, scalar2=None, op0=ALU.mult)
+            nc.vector.tensor_scalar(out=g2x4[:], in0=g2_sb[:, :, 0:4], scalar1=4.0, scalar2=None, op0=ALU.mult)
+
+        def gcopy():
+            nc.vector.tensor_copy(out=g1f[:], in_=g1_sb[:, :, 0:4])
+            nc.vector.tensor_scalar(out=g1f[:], in0=g1f[:], scalar1=-1.0, scalar2=None, op0=ALU.mult)
+
+        def slot(c, tau):
+            return (c * TAU + tau) % 3
+
+        def plv(c, tau):
             lo, hi = CHUNKS[c]
-            new_grp(("e", c, tau))
-            planes = stage.tile([P, 4, 384], BF16, name="planes", bufs=2)
+            tiles[("pl", c, tau)] = tagged([P, 4, 512], BF16, "pl", slot(c, tau))
+            for j in range(4):
+                nc.vector.tensor_scalar(
+                    out=tiles[("pl", c, tau)][:, j, 0 : hi - lo], in0=ratio_sb[:, j, lo + tau : hi + tau],
+                    scalar1=g2x4[:, tau, j : j + 1], scalar2=g2f[:, tau, j : j + 1], op0=ALU.mult, op1=ALU.subtract,
+                )
+
+        def pls(c, tau):
+            lo, hi = CHUNKS[c]
+            tiles[("pl", c, tau)] = tagged([P, 4, 512], BF16, "pl", slot(c, tau))
             for j in range(4):
                 nc.scalar.activation(
-                    out=planes[:, j, 0 : hi - lo], in_=w_il[:, lo + tau : hi + tau, j], func=ACT.Identity,
-                    scale=g2f[:, tau, j : j + 1], bias=g2m[:, tau, j : j + 1],
+                    out=tiles[("pl", c, tau)][:, j, 0 : hi - lo], in_=ratio_sb[:, j, lo + tau : hi + tau], func=ACT.Identity,
+                    scale=g2x4[:, tau, j : j + 1], bias=g2m[:, tau, j : j + 1],
                 )
-            nc.scalar.copy(
-                out=grp[("e", c, tau)][:, 0 : hi - lo, :].rearrange("p (c i) j -> p c j i", i=8),
-                in_=planes[:, :, 0 : hi - lo].rearrange("p j (c i) -> p c j i", i=8),
-            )
 
-        PIECES = {0: ((0, 256), (256, 128)), 1: ((384, 128), (512, 256)), 2: ((768, 256),)}
+        def new_grp(c, tau):
+            if ("eg", c, tau) not in tiles:
+                tiles[("eg", c, tau)] = tagged([P, HALF, 4], BF16, "grp", (c * TAU + tau + 2) % 6)
 
-        def q_eg(c, tau):
+        WBANK = ((4, 5, 6, 7), (4, 5, 6, 7), (4, 5, 6, 7))
+
+        def wv(c, tau, k):
+            i = WBANK[c][(tau + k) % len(WBANK[c])]
+            lo, hi = CHUNKS[c]
+            width = min(256, hi - lo - k * 256)
+            ps = psum.tile([P, 256, 4], BF16, name="bank%d" % i, tag="bank%d" % i)
+            tiles[("wv", c, tau, k)] = ps
+            for q in range(width // P):
+                t0 = k * 256 + q * P
+                nc.tensor.matmul(
+                    ps[:, q * P : (q + 1) * P, :], lhsT=ident16[:],
+                    rhs=tiles[("pl", c, tau)][:, :, t0 : t0 + P].rearrange("p j t -> p t j"), start=True, stop=True,
+                )
+
+        def wvc(c, tau, k):
+            new_grp(c, tau)
+            lo, hi = CHUNKS[c]
+            width = min(256, hi - lo - k * 256)
+            nc.scalar.copy(out=tiles[("eg", c, tau)][:, k * 256 : k * 256 + width, :], in_=tiles[("wv", c, tau, k)][:, 0:width, :])
+
+        def dirv(c, tau):
+            new_grp(c, tau)
+            lo, hi = CHUNKS[c]
+            nc.vector.tensor_copy(out=tiles[("eg", c, tau)][:, 0 : hi - lo, :], in_=tiles[("pl", c, tau)][:, :, 0 : hi - lo].rearrange("p j t -> p t j"))
+
+        def dirs(c, tau):
+            new_grp(c, tau)
+            lo, hi = CHUNKS[c]
+            nc.scalar.copy(out=tiles[("eg", c, tau)][:, 0 : hi - lo, :], in_=tiles[("pl", c, tau)][:, :, 0 : hi - lo].rearrange("p j t -> p t j"))
+
+        def pieces(c):
+            lo, hi = CHUNKS[c]
+            out_list = []
+            while lo < hi:
+                width = max(w for w in (128, 256, 512) if w <= hi - lo)
+                out_list.append((lo, width))
+                lo += width
+            return out_list
+
+        def qe(c, tau):
             base = CHUNKS[c][0]
-            for lo, width in PIECES[c]:
+            for lo, width in pieces(c):
                 quantize(
                     eg_c[:, tau, lo : lo + width], eg_s[:, tau, lo : lo + width],
-                    grp[("e", c, tau)][:, lo - base : lo - base + width, :].rearrange("p t j -> p (t j)"),
+                    tiles[("eg", c, tau)][:, lo - base : lo - base + width, :].rearrange("p t j -> p (t j)"),
                 )
 
-        r_ps = {}
+        RBANK = (0, 0, 4)
 
-        def stage2(c):
-            for lo, width in PIECES[c]:
-                n = lo // HALF
-                if lo % HALF == 0:
-                    for b in range(4):
-                        r_ps[(b, n)] = bank(4 * n + b)
-                for tau in range(TAU):
-                    for b in range(4):
-                        off = lo - n * HALF
-                        mx(r_ps[(b, n)][:, off : off + width], w2_c, w2_s, eg_c, eg_s, b, lo, width, tau)
-
-        REGIONS = {0: ((0, 384),), 1: ((384, 128), (512, 256)), 2: ((768, 256),)}
-        bias = keep.tile([P, 4], F32, name="bias")
-        out_v = out.rearrange("(p b) t -> p b t", b=4)
-        ex = {}
-
-        def exps(c):
-            for lo, width in REGIONS[c]:
-                n = lo // HALF
-                off = lo - n * HALF
-                ex[lo] = stage.tile([P, 4, 384], F32, name="ex", bufs=2)
+        def st2(c, tau):
+            base = CHUNKS[c][0]
+            assert len(pieces(c)) == 1 or tau == 3
+            if tau == 0 or len(pieces(c)) > 1:
                 for b in range(4):
-                    nc.scalar.activation(
-                        out=ex[lo][:, b, 0:width], in_=r_ps[(b, n)][:, off : off + width], func=ACT.Exp, scale=0.5, bias=bias[:, b : b + 1]
-                    )
+                    tiles[("r", b, c)] = bank(RBANK[c] + b)
+            for lo, width in pieces(c):
+                for tt in (range(TAU) if len(pieces(c)) > 1 else (tau,)):
+                    for b in range(4):
+                        mx(tiles[("r", b, c)][:, lo - base : lo - base + width], w2_c, w2_s, eg_c, eg_s, b, lo, width, tt)
 
-        def finish(c):
-            for lo, width in REGIONS[c]:
-                time = (lo + 512) % T
-                for bp in range(2):
-                    bs = slice(2 * bp, 2 * bp + 2)
-                    res = stage.tile([P, 2, 384], F32, name="res", bufs=6)
-                    nc.vector.tensor_tensor(out=res[:, :, 0:width], in0=ex[lo][:, bs, 0:width], in1=h_sb[:, bs, 16 + lo : 16 + lo + width], op=ALU.mult)
-                    nc.sync.dma_start(out=out_v[:, bs, time : time + width], in_=res[:, :, 0:width])
+        out_v = out.rearrange("(p b) t -> p b t", b=4)
 
-        SC, VC = nc.scalar.copy, nc.vector.tensor_copy
-        fills = [(tau, c) for tau in range(1, TAU) for c in range(2)]
-        lo_banks, hi_banks = (0, 1, 2, 3), (4, 5, 6, 7)
+        def exps(c, bp):
+            lo, hi = CHUNKS[c]
+            tiles[("ex", c, bp)] = tagged([P, 2, 512], F32, "ex", (2 * c + bp) % 4)
+            for b2 in range(2):
+                b = 2 * bp + b2
+                nc.scalar.activation(
+                    out=tiles[("ex", c, bp)][:, b2, 0 : hi - lo], in_=tiles[("r", b, c)][:, 0 : hi - lo], func=ACT.Exp,
+                    scale=0.5, bias=bias[:, b : b + 1],
+                )
 
-        def hg_fill(n, i):
-            hg_tensor(n, *fills[i], hi_banks[turns[0] % 4])
-            turns[0] += 1
+        def fin(c, bp):
+            lo, hi = CHUNKS[c]
+            bs = slice(2 * bp, 2 * bp + 2)
+            tiles[("res", c, bp)] = tagged([P, 2, 512], F32, "res", (2 * c + bp) % 3)
+            nc.vector.tensor_tensor(
+                out=tiles[("res", c, bp)][:, :, 0 : hi - lo], in0=tiles[("ex", c, bp)][:, :, 0 : hi - lo],
+                in1=h_sb[:, bs, 16 + lo : 16 + hi], op=ALU.mult,
+            )
 
-        def hg_out(n, i):
-            hg_empty(SC, n, *fills[i])
+        def sto(c, bp):
+            lo, hi = CHUNKS[c]
+            bs = slice(2 * bp, 2 * bp + 2)
+            done = lo
+            while done < hi:
+                end = min(hi, (done // HALF + 1) * HALF)
+                time = (done + 512) % T
+                nc.sync.dma_start(out=out_v[:, bs, time : time + end - done], in_=tiles[("res", c, bp)][:, :, done - lo : end - lo])
+                done = end
 
-        def w1_turn(bp, g):
-            turn("w1", w1_sb[:], g, bp, hi_banks)
-            empty(SC, "w1", g, bp)
-
-        def w2_turn(bp, g, copy):
-            turn("w2", w2_rows[0][:], g, bp, lo_banks)
-            empty(copy, "w2", g, bp)
-
-        def q1(g, bp):
-            q_weight("w1", w1_c, w1_s, g, bp)
-
-        def q2(g, bp):
-            q_weight("w2", w2_c, w2_s, g, bp)
-
-        hg_vector(0, 0)
-        hg_vector(0, 1)
-        for i in range(6):
-            hg_fill(0, i)
-            hg_out(0, i)
-        for tau in range(TAU):
-            q_hg(0, tau)
-        open_s(0)
-        for g in range(TAU):
-            w1_turn(0, g)
-        for g in range(TAU):
-            q1(g, 0)
-        for g in range(TAU):
-            w1_turn(1, g)
-        for tau in range(TAU):
-            stage1(0, tau, 0)
-        hg_vector(1, 0)
-        for g in range(TAU):
-            q1(g, 1)
-        for tau in range(TAU):
-            stage1(0, tau, 1)
-        hg_vector(1, 1)
+        warm(0)
+        warm(1)
+        gcopy()
+        warm(2)
+        hiv(1)
+        hiv(0)
+        hgm(0, 1)
+        w1t(1, 0)
+        hgm(0, 0)
+        w1t(0, 0)
+        w1c(1, 0)
+        hgm(0, 3)
+        w1t(2, 0)
+        w1c(0, 0)
+        qh(0, 0)
+        w1t(3, 0)
+        w1c(2, 0)
+        q1(1, 0)
+        qh(0, 1)
+        his(2)
+        w1t(1, 1)
+        q1(0, 0)
+        qh(0, 3)
+        his(3)
+        st1(0, 0, 0)
+        hgm(0, 2)
+        w1c(3, 0)
+        q1(2, 0)
+        w1t(0, 1)
+        qh(0, 2)
+        hgp(1, 3)
+        hgm(1, 0)
+        w1t(3, 1)
+        st1(0, 1, 0)
+        q1(3, 0)
+        st1(0, 2, 0)
+        qh(1, 0)
+        st1(0, 3, 0)
+        w1c(1, 1)
+        hgm(1, 1)
+        w1t(2, 1)
+        w1c(0, 1)
+        w1c(3, 1)
+        q1(0, 1)
+        st1(1, 0, 0)
+        q1(1, 1)
+        w1c(2, 1)
+        q1(3, 1)
+        st1(0, 0, 1)
+        hgi(1, 3)
+        q1(2, 1)
+        st1(0, 1, 1)
+        hgm(1, 2)
+        st1(0, 2, 1)
+        st1(0, 3, 1)
+        qh(1, 1)
+        st1(1, 0, 1)
+        qh(1, 2)
+        st1(1, 1, 0)
         sig1(0, 0)
+        qh(1, 3)
+        st1(1, 1, 1)
         sig1(0, 1)
-        for i in range(6):
-            hg_fill(1, i)
-        for i in range(3):
-            hg_out(1, i)
-        ln1(0, 0)
-        ln1(0, 1)
-        for i in range(3, 6):
-            hg_out(1, i)
-        q_hg(1, 0)
-        w2_prod(0)
-        q_hg(1, 1)
-        w2_prod(1)
-        w2_prod(2)
-        clamp(0, 0)
-        clamp(0, 1)
-        q_hg(1, 2)
-        q_hg(1, 3)
-        open_s(1)
-        for tau in range(TAU):
-            stage1(1, tau, 0)
-            stage1(1, tau, 1)
-        ln2(0, 0)
-        ln2(0, 1)
-        w2_prod(3)
-        nc.vector.tensor_scalar(out=bias[:], in0=mu_sb[:, 0:4], scalar1=-0.5, scalar2=None, op0=ALU.mult)
-        nc.vector.tensor_scalar(out=g2x4[:], in0=g2_sb[:, :, 0:4], scalar1=4.0, scalar2=None, op0=ALU.mult)
-        nc.vector.tensor_copy(out=g2f[:], in_=g2x4[:])
-        sig2(0, HALF)
+        prod(0)
+        st1(1, 2, 1)
+        sig1(0, 2)
+        st1(1, 3, 1)
+        sig1(0, 3)
+        st1(1, 2, 0)
+        sig1(1, 2)
+        st1(1, 3, 0)
+        sig1(1, 3)
+        prod(3)
         sig1(1, 0)
         sig1(1, 1)
-        turns[0] = 0
-        for g in range(2):
-            w2_turn(0, g, VC)
-        nc.vector.tensor_scalar(out=g2m[:], in0=g2_sb[:, :, 0:4], scalar1=-1.0, scalar2=None, op0=ALU.mult)
-        ratio(0, HALF)
+        ln1(0, 0)
+        prod(1)
+        ln1(0, 1)
+        clamp(0, 0)
+        clamp(0, 1)
         ln1(1, 0)
+        clamp(0, 3)
+        w2t(1, 0)
+        clamp(0, 2)
         ln1(1, 1)
-        q2(0, 0)
-        q2(1, 0)
-        eg_vector(0, 0)
-        eg_vector(0, 1)
-        q_eg(0, 0)
-        for g in range(2, 4):
-            w2_turn(0, g, SC)
-        clamp(1, 0)
         clamp(1, 1)
+        w2t(0, 0)
+        clamp(1, 0)
+        ln2(0, 0)
+        clamp(1, 2)
+        w2t(2, 0)
+        clamp(1, 3)
         ln2(1, 0)
+        prod(2)
+        w2t(3, 0)
+        ln2(0, 1)
         ln2(1, 1)
-        eg_vector(0, 2)
-        q_eg(0, 1)
-        q2(2, 0)
+        w2v(3, 0)
+        w2v(0, 0)
+        sig2(0)
         q2(3, 0)
-        eg_vector(0, 3)
-        q_eg(0, 2)
-        sig2(HALF, T)
-        for g in range(TAU):
-            w2_turn(1, g, SC)
-        q_eg(0, 3)
-        ratio(HALF, T)
-        nc.vector.tensor_copy(out=w_il[:, T : T + 3, :], in_=w_il[:, 0:3, :])
-        eg_scalar(1, 3)
-        eg_vector(1, 0)
-        for g in range(TAU):
-            q2(g, 1)
-        stage2(0)
-        eg_vector(1, 1)
-        q_eg(1, 0)
-        eg_scalar(1, 2)
-        eg_vector(2, 0)
-        q_eg(1, 1)
-        exps(0)
-        eg_scalar(2, 3)
-        eg_vector(2, 1)
-        q_eg(2, 0)
-        q_eg(1, 3)
-        q_eg(1, 2)
-        stage2(1)
-        eg_vector(2, 2)
-        q_eg(2, 1)
-        exps(1)
-        finish(0)
-        q_eg(2, 2)
-        q_eg(2, 3)
-        stage2(2)
-        finish(1)
-        exps(2)
-        finish(2)
+        w2t(0, 1)
+        w2v(1, 0)
+        w2v(2, 0)
+        w2t(3, 1)
+        w2v(0, 1)
+        q2(0, 0)
+        w2t(2, 1)
+        consts()
+        q2(0, 1)
+        q2(1, 0)
+        w2t(1, 1)
+        sig2(1)
+        rat(0)
+        w2c(3, 1)
+        w2c(1, 1)
+        q2(2, 0)
+        plv(0, 2)
+        pls(0, 3)
+        wrap()
+        plv(0, 1)
+        wv(0, 2, 1)
+        rat(1)
+        wv(0, 3, 1)
+        wvc(0, 2, 1)
+        w2c(2, 1)
+        wv(0, 3, 0)
+        wvc(0, 3, 1)
+        wv(0, 1, 1)
+        wvc(0, 3, 0)
+        plv(0, 0)
+        wv(0, 1, 0)
+        wvc(0, 1, 1)
+        pls(1, 3)
+        wv(0, 2, 0)
+        dirv(0, 0)
+        wvc(0, 1, 0)
+        wv(1, 3, 0)
+        plv(1, 1)
+        wvc(0, 2, 0)
+        pls(1, 2)
+        qe(0, 0)
+        wv(1, 1, 0)
+        plv(1, 0)
+        st2(0, 0)
+        pls(2, 3)
+        q2(1, 1)
+        qe(0, 1)
+        wv(1, 2, 0)
+        q2(2, 1)
+        wvc(1, 1, 0)
+        st2(0, 1)
+        qe(0, 2)
+        wvc(1, 3, 0)
+        dirv(1, 0)
+        wvc(1, 2, 0)
+        st2(0, 2)
+        qe(0, 3)
+        pls(2, 2)
+        q2(3, 1)
+        st2(0, 3)
+        qe(1, 3)
+        qe(1, 0)
+        exps(0, 0)
+        plv(2, 1)
+        wv(2, 3, 0)
+        qe(1, 2)
+        wv(2, 2, 0)
+        plv(2, 0)
+        wv(2, 1, 0)
+        qe(1, 1)
+        dirv(2, 0)
+        exps(0, 1)
+        st2(1, 0)
+        fin(0, 0)
+        wvc(2, 2, 0)
+        fin(0, 1)
+        sto(0, 0)
+        st2(1, 1)
+        wvc(2, 3, 0)
+        st2(1, 2)
+        wvc(2, 1, 0)
+        qe(2, 0)
+        st2(1, 3)
+        sto(0, 1)
+        exps(1, 0)
+        qe(2, 1)
+        st2(2, 0)
+        qe(2, 2)
+        exps(1, 1)
+        qe(2, 3)
+        st2(2, 1)
+        fin(1, 0)
+        st2(2, 2)
+        fin(1, 1)
+        sto(1, 0)
+        st2(2, 3)
+        exps(2, 0)
+        sto(1, 1)
+        exps(2, 1)
+        fin(2, 0)
+        fin(2, 1)
+        sto(2, 0)
+        sto(2, 1)

@@ -12,14 +12,18 @@ FP8X4 = mybir.dt.float8_e4m3fn_x4
 ALU = mybir.AluOpType
 ACT = mybir.ActivationFunctionType
 
-F, K, T, TAU = 512, 512, 1024, 4
+F, K, T, TAPS = 512, 512, 1024, 4
 P = 128
-FLOPS = 2 * 2 * F * TAU * K * T
-
-HALF = 512
+J = 4
+BLOCKS = 4
+HALF = T // 2
+QUARTER = T // 4
+PAD = 16
 TINY = 2.0 ** -60
-CHUNKS = ((0, 512), (512, 768), (768, T))
-SIG2 = ((0, 576), (576, T))
+FLOPS = 2 * 2 * F * TAPS * K * T
+
+CHUNKS = ((0, (256, 128)), (384, (256, 128)), (768, (256,)))
+SCALAR_TAP = 3
 
 
 def tile_convolutivenmfexponentiatedupdate_kernel(tc, v, h, w1, g1, w2_bytes, w2_scale, g2, mu, out):
@@ -27,538 +31,422 @@ def tile_convolutivenmfexponentiatedupdate_kernel(tc, v, h, w1, g1, w2_bytes, w2
     with ExitStack() as ctx:
         ctx.enter_context(tc.manual_schedule())
         keep = ctx.enter_context(tc.tile_pool(name="keep", bufs=1))
-        stage = ctx.enter_context(tc.tile_pool(name="stage", bufs=1))
+        stage = ctx.enter_context(tc.tile_pool(name="stage", bufs=4))
         psum = ctx.enter_context(tc.psum_pool(name="psum", bufs=1))
 
-        def bank(i):
-            return psum.tile([P, 512], F32, name="bank%d" % i, tag="bank%d" % i)
+        def bank(i, shape=(P, HALF), dtype=F32):
+            return psum.tile(list(shape), dtype, name="bank%d" % i, tag="bank%d" % i)
 
-        h_sb = keep.tile([P, 4, 16 + T], BF16, name="h_sb", align_bytes=64)
-        w1_sb = keep.tile([P, 4, TAU * K], BF16, name="w1_sb", tag="rows", align_bytes=64)
-        v_sb = keep.tile([P, 4, T], BF16, name="v_sb")
-        w2_by = keep.tile([P, 4, TAU * F], U8, name="w2_by", align_bytes=64)
-        sc_sb = keep.tile([P, TAU * F], F32, name="sc_sb", align_bytes=64)
-        g1_sb = keep.tile([P, TAU, 16], BF16, name="g1_sb")
-        g2_sb = keep.tile([P, TAU, 16], BF16, name="g2_sb")
+        h_sb = keep.tile([P, J, PAD + T], BF16, name="h_sb", align_bytes=64)
+        w1_sb = keep.tile([P, J, TAPS * K], BF16, name="w1_sb", tag="weight_rows", align_bytes=64)
+        v_sb = keep.tile([P, J, T], BF16, name="v_sb")
+        w2_codes_in = keep.tile([P, J, TAPS * F], U8, name="w2_codes_in", align_bytes=64)
+        w2_scale_sb = keep.tile([P, TAPS * F], F32, name="w2_scale_sb", align_bytes=64)
+        g1_sb = keep.tile([P, TAPS, 16], BF16, name="g1_sb")
+        g2_sb = keep.tile([P, TAPS, 16], BF16, name="g2_sb")
         mu_sb = keep.tile([P, 16], BF16, name="mu_sb")
-        wz = keep.tile([P, 256], F32, name="wz")
-        nc.gpsimd.memset(wz[:], 0.0)
-        h_v = h.rearrange("(p j) t -> p j t", j=4)
-        v_v = v.rearrange("(p j) t -> p j t", j=4)
-        w1_v = w1.rearrange("(m b) k -> m b k", b=4)
-        w2_v = w2_bytes.rearrange("(m b) k -> m b k", b=4)
-        nc.scalar.dma_start(out=g1_sb[:, :, 0:4], in_=g1.rearrange("(a p j) -> p a j", a=TAU, j=4))
-        nc.sync.dma_start(out=h_sb[:, :, 12:528], in_=h_v[:, :, 508:T])
-        for b in range(0, 4, 2):
-            nc.sync.dma_start(out=w1_sb[:, b : b + 2, :], in_=w1_v[:, b : b + 2, :])
-        nc.sync.dma_start(out=h_sb[:, :, 528:1040], in_=h_v[:, :, 0:512])
-        for b in range(0, 4, 2):
-            nc.sync.dma_start(out=w2_by[:, b : b + 2, :], in_=w2_v[:, b : b + 2, :])
-        nc.sync.dma_start(out=sc_sb[:], in_=w2_scale.rearrange("o k -> (o k)").partition_broadcast(P))
-        nc.sync.dma_start(out=v_sb[:, :, 0:512], in_=v_v[:, :, 512:T])
-        nc.sync.dma_start(out=v_sb[:, :, 512:T], in_=v_v[:, :, 0:512])
-        nc.scalar.dma_start(out=g2_sb[:, :, 0:4], in_=g2.rearrange("(a p j) -> p a j", a=TAU, j=4))
-        nc.scalar.dma_start(out=mu_sb[:, 0:4], in_=mu.rearrange("(p j) -> p j", j=4))
+        h_rows = h.rearrange("(p j) t -> p j t", j=J)
+        v_rows = v.rearrange("(p j) t -> p j t", j=J)
+        w1_rows = w1.rearrange("(m b) k -> m b k", b=BLOCKS)
+        w2_rows = w2_bytes.rearrange("(m b) k -> m b k", b=BLOCKS)
+        nc.scalar.dma_start(out=g1_sb[:, :, 0:J], in_=g1.rearrange("(a p j) -> p a j", a=TAPS, j=J))
+        mid = PAD + QUARTER
+        nc.sync.dma_start(out=h_sb[:, :, PAD - TAPS : mid], in_=h_rows[:, :, HALF - TAPS : HALF + QUARTER])
+        nc.sync.dma_start(out=h_sb[:, :, mid : PAD + HALF], in_=h_rows[:, :, HALF + QUARTER : T])
+        for b in range(0, BLOCKS, 2):
+            nc.sync.dma_start(out=w1_sb[:, b : b + 2, :], in_=w1_rows[:, b : b + 2, :])
+        nc.sync.dma_start(out=h_sb[:, :, PAD + HALF : PAD + T], in_=h_rows[:, :, 0:HALF])
+        nc.sync.dma_start(out=w2_codes_in[:, 0:2, :], in_=w2_rows[:, 0:2, :])
+        nc.sync.dma_start(out=w2_scale_sb[:], in_=w2_scale.rearrange("o k -> (o k)").partition_broadcast(P))
+        nc.sync.dma_start(out=w2_codes_in[:, 2:4, :], in_=w2_rows[:, 2:4, :])
+        nc.sync.dma_start(out=v_sb[:, :, 0:HALF], in_=v_rows[:, :, HALF:T])
+        nc.sync.dma_start(out=v_sb[:, :, HALF:T], in_=v_rows[:, :, 0:HALF])
+        nc.sync.dma_start(out=g2_sb[:, :, 0:J], in_=g2.rearrange("(a p j) -> p a j", a=TAPS, j=J))
+        nc.sync.dma_start(out=mu_sb[:, 0:J], in_=mu.rearrange("(p j) -> p j", j=J))
 
         ident = keep.tile([P, P], F32, name="ident")
         make_identity(nc, ident[:])
         ident16 = keep.tile([P, P], BF16, name="ident16")
         make_identity(nc, ident16[:])
+        zeros = keep.tile([P, QUARTER], F32, name="zeros")
+        nc.gpsimd.memset(zeros[:], 0.0)
         dummy = keep.tile([P, 2], F32, name="dummy")
         nc.vector.memset(dummy[:], 0.0)
         nc.scalar.activation(out=dummy[:, 1:2], in_=dummy[:, 0:1], func=ACT.Sigmoid)
 
-        g1n = keep.tile([P, TAU, 4], BF16, name="g1n")
-        nc.vector.tensor_scalar(out=g1n[:], in0=g1_sb[:, :, 0:4], scalar1=-1.0, scalar2=None, op0=ALU.mult)
-        h_il = keep.tile([P, 16 + T, 4], BF16, name="h_il", align_bytes=64)
-        hg_c = keep.tile([P, TAU, T], U32, name="hg_c", align_bytes=64)
-        hg_s = keep.tile([P, TAU, T], U8, name="hg_s", align_bytes=64)
-        eg_c = keep.tile([P, TAU, T], U32, name="eg_c", align_bytes=64)
-        eg_s = keep.tile([P, TAU, T], U8, name="eg_s", align_bytes=64)
-        w1_c = keep.tile([P, TAU, 512], U32, name="w1_c", align_bytes=64)
-        w1_s = keep.tile([P, TAU, 512], U8, name="w1_s", align_bytes=64)
-        w2_c = keep.tile([P, TAU, 512], U32, name="w2_c", align_bytes=64)
-        w2_s = keep.tile([P, TAU, 512], U8, name="w2_s", align_bytes=64)
-        mid = keep.tile([P, 4, T], F32, name="mid", align_bytes=64)
-        ratio_sb = keep.tile([P, 4, T + 16], F32, name="ratio_sb", align_bytes=64)
+        g1_neg = keep.tile([P, TAPS, J], BF16, name="g1_neg")
+        nc.vector.tensor_scalar(out=g1_neg[:], in0=g1_sb[:, :, 0:J], scalar1=-1.0, scalar2=None, op0=ALU.mult)
+        g2_neg = keep.tile([P, TAPS, J], F32, name="g2_neg")
+        g2_four = keep.tile([P, TAPS, J], F32, name="g2_four")
+        g2_four16 = keep.tile([P, TAPS, J], BF16, name="g2_four16")
+        mu_half = keep.tile([P, J], F32, name="mu_half")
 
+        def second_constants():
+            nc.vector.tensor_scalar(out=mu_half[:], in0=mu_sb[:, 0:J], scalar1=-0.5, scalar2=None, op0=ALU.mult)
+            nc.vector.tensor_scalar(out=g2_neg[:], in0=g2_sb[:, :, 0:J], scalar1=-1.0, scalar2=None, op0=ALU.mult)
+            nc.vector.tensor_scalar(out=g2_four16[:], in0=g2_sb[:, :, 0:J], scalar1=4.0, scalar2=None, op0=ALU.mult)
+            nc.vector.tensor_scalar(out=g2_four[:], in0=g2_sb[:, :, 0:J], scalar1=4.0, scalar2=None, op0=ALU.mult)
 
-        chunks = len(CHUNKS)
+        def operand(name, width):
+            return (
+                keep.tile([P, TAPS, width], U32, name=name + "_codes", align_bytes=64),
+                keep.tile([P, TAPS, width], U8, name=name + "_scales", align_bytes=64),
+            )
 
-        def tagged(shape, dt, name, slot):
-            return stage.tile(shape, dt, name="%s%d" % (name, slot), tag="%s%d" % (name, slot), align_bytes=64)
+        hg_q, w1_q, eg_q, w2_q = operand("hg", T), operand("w1", F), operand("eg", T), operand("w2", K)
+        h_il = keep.tile([P, PAD + T, J], BF16, name="h_il", align_bytes=64)
+        diag = keep.tile([P, TAPS, J, P], BF16, name="diag")
+        act = keep.tile([P, BLOCKS, T], F32, name="act", align_bytes=64)
+        ratio = keep.tile([P, T + TAPS, J], F32, name="ratio", align_bytes=64)
 
-        def quantize(codes, scales, grouped):
-            nc.vector.quantize_mx(out=codes.bitcast(FP8X4), scales=scales, in_=grouped)
+        def quantize(operand_q, tap, lo, width, grouped):
+            codes, scales = operand_q
+            nc.vector.quantize_mx(
+                out=codes[:, tap, lo : lo + width].bitcast(FP8X4),
+                scales=scales[:, tap, lo : lo + width],
+                in_=grouped.rearrange("p c j -> p (c j)"),
+            )
 
-        def cols(n):
+        def multiply(ps, weight_q, moving_q, b, tap, lo, width):
+            rows, columns = slice(b * P, (b + 1) * P), slice(lo, lo + width)
+            nc.tensor.matmul_mx(
+                out=ps,
+                lhsT=weight_q[0][:, tap, rows].bitcast(FP8X4),
+                lhsT_scale=weight_q[1][:, tap, rows],
+                rhs=moving_q[0][:, tap, columns].bitcast(FP8X4),
+                rhs_scale=moving_q[1][:, tap, columns],
+                start=(tap == 0),
+                stop=(tap == TAPS - 1),
+            )
+
+        def warm():
+            nc.tensor.matmul(bank(0)[:, 0:QUARTER], lhsT=ident[:], rhs=zeros[:], start=True, stop=True)
+
+        turned, grouped_w = {}, {}
+
+        def turn(name, rows_sb, tap, pair, i):
+            words = rows_sb.bitcast(F32)
+            ps = bank(i, (P, 2, 2, P))
+            for b in range(2):
+                for u in range(2):
+                    start = tap * (K // 2) + u
+                    nc.tensor.transpose(ps[:, b, u, :], words[:, 2 * pair + b, start : (tap + 1) * (K // 2) : 2], ident[:])
+            turned[name, tap, pair] = ps
+
+        def empty(name, tap, pair):
+            if (name, tap) not in grouped_w:
+                grouped_w[name, tap] = stage.tile([P, BLOCKS * P, J], BF16, name="grouped_w", align_bytes=64)
+            part = grouped_w[name, tap][:, pair * 2 * P : (pair + 1) * 2 * P, :].rearrange("p m j -> p (m j)").bitcast(F32)
+            nc.scalar.copy(
+                out=part.rearrange("p (b m u) -> p b m u", b=2, u=2),
+                in_=turned[name, tap, pair][:].rearrange("p b u m -> p b m u"),
+            )
+
+        def quantize_w(name, weight_q, tap, pair):
+            lo = pair * 2 * P
+            quantize(weight_q, tap, lo, 2 * P, grouped_w[name, tap][:, lo : lo + 2 * P, :])
+
+        grouped = {}
+
+        def grouped_tile(key):
+            grouped[key] = stage.tile([P, HALF, J], BF16, name="grouped", align_bytes=64, bufs=6)
+            return grouped[key]
+
+        def interleave_h(copy, lo, hi):
+            copy(out=h_il[:, lo:hi, :], in_=h_sb[:, :, lo:hi].rearrange("p j t -> p t j"))
+
+        def make_diag(tap):
+            for j in range(J):
+                nc.vector.tensor_scalar(
+                    out=diag[:, tap, j, :], in0=ident16[:], scalar1=g1_neg[:, tap, j : j + 1], scalar2=None, op0=ALU.mult
+                )
+
+        def hg_vector(n, tap):
+            lo = PAD + n * HALF - tap
+            nc.vector.tensor_tensor(
+                out=grouped_tile(("hg", n, tap))[:],
+                in0=h_il[:, lo : lo + HALF, :],
+                in1=g1_neg[:, tap, :].unsqueeze(1).to_broadcast([P, HALF, J]),
+                op=ALU.mult,
+            )
+
+        hg_banks = {}
+
+        def hg_tensor(n, tap, quarter, i):
+            lo = PAD + n * HALF + quarter * QUARTER - tap
+            ps = bank(i, (P, J, QUARTER), BF16)
+            for j in range(J):
+                nc.tensor.matmul(ps[:, j, :], lhsT=diag[:, tap, j, :], rhs=h_sb[:, j, lo : lo + QUARTER], start=True, stop=True)
+            hg_banks[n, tap, quarter] = ps
+
+        def hg_interleave(n, tap, quarter):
+            tile = grouped_tile(("hg", n, tap)) if quarter == 0 else grouped["hg", n, tap]
+            nc.scalar.copy(
+                out=tile[:, quarter * QUARTER : (quarter + 1) * QUARTER, :],
+                in_=hg_banks[n, tap, quarter][:].rearrange("p j t -> p t j"),
+            )
+
+        def quantize_hg(n, tap):
+            quantize(hg_q, tap, n * HALF, HALF, grouped["hg", n, tap][:])
+
+        s_banks = {}
+
+        def stage1(n, tap, pair):
+            for b in range(2 * pair, 2 * pair + 2):
+                if tap == 0:
+                    s_banks[n, b] = bank(n * BLOCKS + b)
+                multiply(s_banks[n, b][:], w1_q, hg_q, b, tap, n * HALF, HALF)
+
+        def half(n):
             return slice(n * HALF, (n + 1) * HALF)
 
-        HI = ((12, 272), (272, 528), (528, 784), (784, 1040))
+        def sigmoid_s(n):
+            for b in range(BLOCKS):
+                nc.scalar.activation(out=act[:, b, half(n)], in_=s_banks[n, b][:], func=ACT.Sigmoid)
 
-        def hiv(k):
-            lo, hi = HI[k]
-            nc.vector.tensor_copy(out=h_il[:, lo:hi, :], in_=h_sb[:, :, lo:hi].rearrange("p j t -> p t j"))
+        def log(n, scale):
+            for pair in range(2):
+                part = act[:, 2 * pair : 2 * pair + 2, half(n)]
+                nc.scalar.activation(out=part, in_=part, func=ACT.Ln, scale=scale, bias=TINY)
 
-        def his(k):
-            lo, hi = HI[k]
-            nc.scalar.copy(out=h_il[:, lo:hi, :], in_=h_sb[:, :, lo:hi].rearrange("p j t -> p t j"))
+        def clamp(n):
+            for b in range(BLOCKS):
+                part = act[:, b, half(n)]
+                nc.vector.scalar_tensor_tensor(out=part, in0=s_banks[n, b][:], scalar=0.0, in1=part, op0=ALU.min, op1=ALU.min)
 
-        wp = psum.tile([P, 512], F32, name="warm", tag="bank0")
+        def sigmoid_log(n):
+            nc.scalar.activation(out=act[:, :, half(n)], in_=act[:, :, half(n)], func=ACT.Sigmoid, scale=-1.0)
 
-        def warm(k):
-            nc.tensor.matmul(wp[:, 0:256], lhsT=ident[:], rhs=wz[:], start=True, stop=True)
-
-        tiles = {}
-
-        def turn(which, src, g, bp, i):
-            ps = bank(i)
-            tiles[("ps", which, g, bp)] = ps
-            words = src.bitcast(F32)
-            for b2 in range(2):
-                for u in range(2):
-                    col = (b2 * 2 + u) * P
-                    nc.tensor.transpose(ps[:, col : col + P], words[:, bp * 2 + b2, 256 * g + u : 256 * (g + 1) : 2], ident[:])
-
-        def empty(copy, which, g, bp):
-            if ("wt", which, g) not in tiles:
-                tiles[("wt", which, g)] = tagged([P, 512, 4], BF16, "wt", g)
-            dst = tiles[("wt", which, g)][:, bp * 256 : (bp + 1) * 256, :].rearrange("p m j -> p (m j)").bitcast(F32)
-            copy(
-                out=dst.rearrange("p (b m u) -> p b m u", b=2, u=2),
-                in_=tiles[("ps", which, g, bp)][:].rearrange("p (b u m) -> p b m u", b=2, u=2),
-            )
-
-        def w1t(g, bp):
-            turn("w1", w1_sb[:], g, bp, 4 + g)
-
-        def w1c(g, bp):
-            empty(nc.scalar.copy, "w1", g, bp)
-
-        def w1v(g, bp):
-            empty(nc.vector.tensor_copy, "w1", g, bp)
-
-        def w2t(g, bp):
-            turn("w2", tiles["w2"][:], g, bp, g)
-
-        def w2c(g, bp):
-            empty(nc.scalar.copy, "w2", g, bp)
-
-        def w2v(g, bp):
-            empty(nc.vector.tensor_copy, "w2", g, bp)
-
-        def q_weight(which, codes, scales, g, bp):
-            ms = slice(bp * 256, (bp + 1) * 256)
-            quantize(codes[:, g, ms], scales[:, g, ms], tiles[("wt", which, g)][:, ms, :].rearrange("p m j -> p (m j)"))
-
-        def q1(g, bp):
-            q_weight("w1", w1_c, w1_s, g, bp)
-
-        def q2(g, bp):
-            q_weight("w2", w2_c, w2_s, g, bp)
-
-        def hgm(n, tau):
-            tiles[("hg", n, tau)] = tagged([P, HALF, 4], BF16, "grp", (n * TAU + tau) % 6)
-            lo = 16 + n * HALF - tau
+        def make_ratio(n):
             nc.vector.tensor_tensor(
-                out=tiles[("hg", n, tau)][:], in0=h_il[:, lo : lo + HALF, :],
-                in1=g1n[:, tau, :].unsqueeze(1).to_broadcast([P, HALF, 4]), op=ALU.mult,
+                out=ratio[:, half(n), :].rearrange("p (c i) b -> p c b i", i=4),
+                in0=act[:, :, half(n)].rearrange("p b (c i) -> p c b i", i=4),
+                in1=v_sb[:, :, half(n)].rearrange("p b (c i) -> p c b i", i=4),
+                op=ALU.mult,
             )
 
-        g1f = keep.tile([P, TAU, 4], F32, name="g1f")
+        def wrap_ratio():
+            nc.vector.tensor_copy(out=ratio[:, T : T + TAPS - 1, :], in_=ratio[:, 0 : TAPS - 1, :])
 
-        def hgp(n, tau):
-            tiles[("hp", n, tau)] = tagged([P, 4, 512], BF16, "pl", 3)
-            lo = 16 + n * HALF - tau
-            for j in range(4):
-                nc.scalar.activation(out=tiles[("hp", n, tau)][:, j, :], in_=h_sb[:, j, lo : lo + HALF], func=ACT.Copy, scale=g1f[:, tau, j : j + 1])
+        w2_sb = []
 
-        def hgi(n, tau):
-            tiles[("hg", n, tau)] = tagged([P, HALF, 4], BF16, "grp", (n * TAU + tau) % 6)
-            nc.scalar.copy(out=tiles[("hg", n, tau)][:], in_=tiles[("hp", n, tau)][:].rearrange("p j t -> p t j"))
-
-        def qh(n, tau):
-            quantize(hg_c[:, tau, cols(n)], hg_s[:, tau, cols(n)], tiles[("hg", n, tau)][:].rearrange("p t j -> p (t j)"))
-
-        def mx(ps, wc, ws, xc, xs, b, lo, width, tau):
-            bs = slice(b * P, (b + 1) * P)
-            cs = slice(lo, lo + width)
-            nc.tensor.matmul_mx(
-                out=ps, lhsT=wc[:, tau, bs].bitcast(FP8X4), lhsT_scale=ws[:, tau, bs],
-                rhs=xc[:, tau, cs].bitcast(FP8X4), rhs_scale=xs[:, tau, cs], start=(tau == 0), stop=(tau == TAU - 1),
+        def scale_w2(b):
+            if not w2_sb:
+                w2_sb.append(keep.tile([P, J, TAPS * F], BF16, name="w2_sb", tag="weight_rows", align_bytes=64))
+            nc.vector.tensor_tensor(
+                out=w2_sb[0][:, b, :], in0=w2_codes_in[:, b, :].bitcast(FP8), in1=w2_scale_sb[:], op=ALU.mult
             )
 
-        def st1(n, tau, bp):
-            for b in range(2 * bp, 2 * bp + 2):
-                if tau == 0:
-                    tiles[("s", b, n)] = bank(4 * n + b)
-                mx(tiles[("s", b, n)][:], w1_c, w1_s, hg_c, hg_s, b, n * HALF, HALF, tau)
+        def turn_w2(tap, pair):
+            turn("w2", w2_sb[0][:], tap, pair, tap % 2)
+            empty("w2", tap, pair)
 
-        def sig1(n, b):
-            nc.scalar.activation(out=mid[:, b, cols(n)], in_=tiles[("s", b, n)][:], func=ACT.Sigmoid)
+        def columns(c):
+            return CHUNKS[c][0], CHUNKS[c][0] + sum(CHUNKS[c][1])
 
-        def ln1(n, bp):
-            sl = mid[:, 2 * bp : 2 * bp + 2, cols(n)]
-            nc.scalar.activation(out=sl, in_=sl, func=ACT.Ln, bias=TINY)
-
-        def clamp(n, b):
+        def eg_vector(c, tap):
+            lo, hi = columns(c)
             nc.vector.scalar_tensor_tensor(
-                out=mid[:, b, cols(n)], in0=tiles[("s", b, n)][:], scalar=0.0, in1=mid[:, b, cols(n)], op0=ALU.min, op1=ALU.min
+                out=grouped_tile(("eg", c, tap))[:, 0 : hi - lo, :],
+                in0=ratio[:, lo + tap : hi + tap, :],
+                scalar=0.25,
+                in1=g2_four16[:, tap, :].unsqueeze(1).to_broadcast([P, hi - lo, J]),
+                op0=ALU.subtract,
+                op1=ALU.mult,
             )
 
-        def ln2(n, bp):
-            sl = mid[:, 2 * bp : 2 * bp + 2, cols(n)]
-            nc.scalar.activation(out=sl, in_=sl, func=ACT.Ln, scale=-4.0, bias=TINY)
-
-        def sig2(k):
-            lo, hi = SIG2[k]
-            nc.scalar.activation(out=mid[:, :, lo:hi], in_=mid[:, :, lo:hi], func=ACT.Sigmoid, scale=-1.0)
-
-        def prod(b):
-            if "w2" not in tiles:
-                tiles["w2"] = keep.tile([P, 4, TAU * F], BF16, name="w2_sb", tag="rows", align_bytes=64)
-            nc.vector.tensor_tensor(out=tiles["w2"][:, b, :], in0=w2_by[:, b, :].bitcast(FP8), in1=sc_sb[:], op=ALU.mult)
-
-        def rat(k):
-            lo, hi = SIG2[k]
-            nc.vector.tensor_tensor(out=ratio_sb[:, :, lo:hi], in0=mid[:, :, lo:hi], in1=v_sb[:, :, lo:hi], op=ALU.mult)
-
-        def wrap():
-            nc.vector.tensor_copy(out=ratio_sb[:, :, T : T + 3], in_=ratio_sb[:, :, 0:3])
-
-        g2f = keep.tile([P, TAU, 4], F32, name="g2f")
-        g2m = keep.tile([P, TAU, 4], F32, name="g2m")
-        g2x4 = keep.tile([P, TAU, 4], F32, name="g2x4")
-        bias = keep.tile([P, 4], F32, name="bias")
-
-        def consts():
-            nc.vector.tensor_scalar(out=bias[:], in0=mu_sb[:, 0:4], scalar1=-0.5, scalar2=None, op0=ALU.mult)
-            nc.vector.tensor_copy(out=g2f[:], in_=g2_sb[:, :, 0:4])
-            nc.vector.tensor_scalar(out=g2m[:], in0=g2_sb[:, :, 0:4], scalar1=-1.0, scalar2=None, op0=ALU.mult)
-            nc.vector.tensor_scalar(out=g2x4[:], in0=g2_sb[:, :, 0:4], scalar1=4.0, scalar2=None, op0=ALU.mult)
-
-        def gcopy():
-            nc.vector.tensor_copy(out=g1f[:], in_=g1_sb[:, :, 0:4])
-            nc.vector.tensor_scalar(out=g1f[:], in0=g1f[:], scalar1=-1.0, scalar2=None, op0=ALU.mult)
-
-        def slot(c, tau):
-            return (c * TAU + tau) % 3
-
-        def plv(c, tau):
-            lo, hi = CHUNKS[c]
-            tiles[("pl", c, tau)] = tagged([P, 4, 512], BF16, "pl", slot(c, tau))
-            for j in range(4):
-                nc.vector.tensor_scalar(
-                    out=tiles[("pl", c, tau)][:, j, 0 : hi - lo], in0=ratio_sb[:, j, lo + tau : hi + tau],
-                    scalar1=g2x4[:, tau, j : j + 1], scalar2=g2f[:, tau, j : j + 1], op0=ALU.mult, op1=ALU.subtract,
-                )
-
-        def pls(c, tau):
-            lo, hi = CHUNKS[c]
-            tiles[("pl", c, tau)] = tagged([P, 4, 512], BF16, "pl", slot(c, tau))
-            for j in range(4):
+        def eg_scalar(c, tap):
+            lo, hi = columns(c)
+            rows = stage.tile([P, J, HALF], BF16, name="eg_rows", align_bytes=64, bufs=2)
+            for j in range(J):
                 nc.scalar.activation(
-                    out=tiles[("pl", c, tau)][:, j, 0 : hi - lo], in_=ratio_sb[:, j, lo + tau : hi + tau], func=ACT.Identity,
-                    scale=g2x4[:, tau, j : j + 1], bias=g2m[:, tau, j : j + 1],
+                    out=rows[:, j, 0 : hi - lo],
+                    in_=ratio[:, lo + tap : hi + tap, j],
+                    func=ACT.Identity,
+                    scale=g2_four[:, tap, j : j + 1],
+                    bias=g2_neg[:, tap, j : j + 1],
                 )
-
-        def new_grp(c, tau):
-            if ("eg", c, tau) not in tiles:
-                tiles[("eg", c, tau)] = tagged([P, HALF, 4], BF16, "grp", (c * TAU + tau + 2) % 6)
-
-        WBANK = ((4, 5, 6, 7), (4, 5, 6, 7), (4, 5, 6, 7))
-
-        def wv(c, tau, k):
-            i = WBANK[c][(tau + k) % len(WBANK[c])]
-            lo, hi = CHUNKS[c]
-            width = min(256, hi - lo - k * 256)
-            ps = psum.tile([P, 256, 4], BF16, name="bank%d" % i, tag="bank%d" % i)
-            tiles[("wv", c, tau, k)] = ps
-            for q in range(width // P):
-                t0 = k * 256 + q * P
-                nc.tensor.matmul(
-                    ps[:, q * P : (q + 1) * P, :], lhsT=ident16[:],
-                    rhs=tiles[("pl", c, tau)][:, :, t0 : t0 + P].rearrange("p j t -> p t j"), start=True, stop=True,
-                )
-
-        def wvc(c, tau, k):
-            new_grp(c, tau)
-            lo, hi = CHUNKS[c]
-            width = min(256, hi - lo - k * 256)
-            nc.scalar.copy(out=tiles[("eg", c, tau)][:, k * 256 : k * 256 + width, :], in_=tiles[("wv", c, tau, k)][:, 0:width, :])
-
-        def dirv(c, tau):
-            new_grp(c, tau)
-            lo, hi = CHUNKS[c]
-            nc.vector.tensor_copy(out=tiles[("eg", c, tau)][:, 0 : hi - lo, :], in_=tiles[("pl", c, tau)][:, :, 0 : hi - lo].rearrange("p j t -> p t j"))
-
-        def dirs(c, tau):
-            new_grp(c, tau)
-            lo, hi = CHUNKS[c]
-            nc.scalar.copy(out=tiles[("eg", c, tau)][:, 0 : hi - lo, :], in_=tiles[("pl", c, tau)][:, :, 0 : hi - lo].rearrange("p j t -> p t j"))
+            nc.scalar.copy(out=grouped_tile(("eg", c, tap))[:, 0 : hi - lo, :], in_=rows[:, :, 0 : hi - lo].rearrange("p j t -> p t j"))
 
         def pieces(c):
-            lo, hi = CHUNKS[c]
-            out_list = []
-            while lo < hi:
-                width = max(w for w in (128, 256, 512) if w <= hi - lo)
-                out_list.append((lo, width))
+            lo, list_of_pieces = CHUNKS[c][0], []
+            for width in CHUNKS[c][1]:
+                list_of_pieces.append((lo, width))
                 lo += width
-            return out_list
+            return list_of_pieces
 
-        def qe(c, tau):
-            base = CHUNKS[c][0]
+        def quantize_eg(c, tap):
+            first = CHUNKS[c][0]
             for lo, width in pieces(c):
-                quantize(
-                    eg_c[:, tau, lo : lo + width], eg_s[:, tau, lo : lo + width],
-                    tiles[("eg", c, tau)][:, lo - base : lo - base + width, :].rearrange("p t j -> p (t j)"),
-                )
+                quantize(eg_q, tap, lo, width, grouped["eg", c, tap][:, lo - first : lo - first + width, :])
 
-        RBANK = (0, 0, 4)
+        r_banks, grown = {}, {}
 
-        def st2(c, tau):
-            base = CHUNKS[c][0]
-            assert len(pieces(c)) == 1 or tau == 3
-            if tau == 0 or len(pieces(c)) > 1:
-                for b in range(4):
-                    tiles[("r", b, c)] = bank(RBANK[c] + b)
+        def stage2(c, first_bank):
+            first = CHUNKS[c][0]
+            for b in range(BLOCKS):
+                r_banks[c, b] = bank(first_bank + b)
             for lo, width in pieces(c):
-                for tt in (range(TAU) if len(pieces(c)) > 1 else (tau,)):
-                    for b in range(4):
-                        mx(tiles[("r", b, c)][:, lo - base : lo - base + width], w2_c, w2_s, eg_c, eg_s, b, lo, width, tt)
+                for tap in range(TAPS):
+                    for b in range(BLOCKS):
+                        multiply(r_banks[c, b][:, lo - first : lo - first + width], w2_q, eg_q, b, tap, lo, width)
 
-        out_v = out.rearrange("(p b) t -> p b t", b=4)
-
-        def exps(c, bp):
-            lo, hi = CHUNKS[c]
-            tiles[("ex", c, bp)] = tagged([P, 2, 512], F32, "ex", (2 * c + bp) % 4)
-            for b2 in range(2):
-                b = 2 * bp + b2
+        def exponential(c, pair):
+            lo, hi = columns(c)
+            grown[c, pair] = stage.tile([P, 2, HALF], F32, name="grown")
+            for b in range(2):
+                block = 2 * pair + b
                 nc.scalar.activation(
-                    out=tiles[("ex", c, bp)][:, b2, 0 : hi - lo], in_=tiles[("r", b, c)][:, 0 : hi - lo], func=ACT.Exp,
-                    scale=0.5, bias=bias[:, b : b + 1],
+                    out=grown[c, pair][:, b, 0 : hi - lo],
+                    in_=r_banks[c, block][:, 0 : hi - lo],
+                    func=ACT.Exp,
+                    scale=0.5,
+                    bias=mu_half[:, block : block + 1],
                 )
 
-        def fin(c, bp):
-            lo, hi = CHUNKS[c]
-            bs = slice(2 * bp, 2 * bp + 2)
-            tiles[("res", c, bp)] = tagged([P, 2, 512], F32, "res", (2 * c + bp) % 3)
+        out_rows = out.rearrange("(p b) t -> p b t", b=BLOCKS)
+
+        def finish(c, pair):
+            lo, hi = columns(c)
+            rows = slice(2 * pair, 2 * pair + 2)
+            result = stage.tile([P, 2, HALF], F32, name="result")
             nc.vector.tensor_tensor(
-                out=tiles[("res", c, bp)][:, :, 0 : hi - lo], in0=tiles[("ex", c, bp)][:, :, 0 : hi - lo],
-                in1=h_sb[:, bs, 16 + lo : 16 + hi], op=ALU.mult,
+                out=result[:, :, 0 : hi - lo],
+                in0=grown[c, pair][:, :, 0 : hi - lo],
+                in1=h_sb[:, rows, PAD + lo : PAD + hi],
+                op=ALU.mult,
             )
+            for a, z in ((lo, min(hi, HALF)), (max(lo, HALF), hi)):
+                if a < z:
+                    time = (a + HALF) % T
+                    nc.sync.dma_start(out=out_rows[:, rows, time : time + z - a], in_=result[:, :, a - lo : z - lo])
 
-        def sto(c, bp):
-            lo, hi = CHUNKS[c]
-            bs = slice(2 * bp, 2 * bp + 2)
-            done = lo
-            while done < hi:
-                end = min(hi, (done // HALF + 1) * HALF)
-                time = (done + 512) % T
-                nc.sync.dma_start(out=out_v[:, bs, time : time + end - done], in_=tiles[("res", c, bp)][:, :, done - lo : end - lo])
-                done = end
+        make_diag(3)
+        interleave_h(nc.vector.tensor_copy, PAD - TAPS, PAD + QUARTER)
+        interleave_h(nc.vector.tensor_copy, PAD + QUARTER, PAD + HALF)
+        make_diag(2)
+        for quarter in range(2):
+            hg_tensor(0, 3, quarter, 2 + quarter)
+            hg_interleave(0, 3, quarter)
+        warm()
+        hg_vector(0, 0)
+        hg_vector(0, 1)
+        for tap in range(TAPS):
+            turn("w1", w1_sb[:], tap, 0, 4 + tap)
+            empty("w1", tap, 0)
+            if tap % 2 == 1:
+                warm()
+        quantize_hg(0, 3)
+        quantize_w("w1", w1_q, 0, 0)
+        hg_vector(0, 2)
+        for tap in range(1, TAPS):
+            quantize_w("w1", w1_q, tap, 0)
+        interleave_h(nc.scalar.copy, PAD + HALF, PAD + HALF + QUARTER)
+        for tap in range(TAPS):
+            turn("w1", w1_sb[:], tap, 1, 4 + tap)
+            empty("w1", tap, 1)
+            if tap % 2 == 1:
+                warm()
+        interleave_h(nc.vector.tensor_copy, PAD + HALF + QUARTER, PAD + T)
+        for tap in range(3):
+            quantize_hg(0, tap)
 
-        warm(0)
-        warm(1)
-        gcopy()
-        warm(2)
-        hiv(1)
-        hiv(0)
-        hgm(0, 1)
-        w1t(1, 0)
-        hgm(0, 0)
-        w1t(0, 0)
-        w1c(1, 0)
-        hgm(0, 3)
-        w1t(2, 0)
-        w1c(0, 0)
-        qh(0, 0)
-        w1t(3, 0)
-        w1c(2, 0)
-        q1(1, 0)
-        qh(0, 1)
-        his(2)
-        w1t(1, 1)
-        q1(0, 0)
-        qh(0, 3)
-        his(3)
-        st1(0, 0, 0)
-        hgm(0, 2)
-        w1c(3, 0)
-        q1(2, 0)
-        w1t(0, 1)
-        qh(0, 2)
-        hgp(1, 3)
-        hgm(1, 0)
-        w1t(3, 1)
-        st1(0, 1, 0)
-        q1(3, 0)
-        st1(0, 2, 0)
-        qh(1, 0)
-        st1(0, 3, 0)
-        w1c(1, 1)
-        hgm(1, 1)
-        w1t(2, 1)
-        w1c(0, 1)
-        w1c(3, 1)
-        q1(0, 1)
-        st1(1, 0, 0)
-        q1(1, 1)
-        w1c(2, 1)
-        q1(3, 1)
-        st1(0, 0, 1)
-        hgi(1, 3)
-        q1(2, 1)
-        st1(0, 1, 1)
-        hgm(1, 2)
-        st1(0, 2, 1)
-        st1(0, 3, 1)
-        qh(1, 1)
-        st1(1, 0, 1)
-        qh(1, 2)
-        st1(1, 1, 0)
-        sig1(0, 0)
-        qh(1, 3)
-        st1(1, 1, 1)
-        sig1(0, 1)
-        prod(0)
-        st1(1, 2, 1)
-        sig1(0, 2)
-        st1(1, 3, 1)
-        sig1(0, 3)
-        st1(1, 2, 0)
-        sig1(1, 2)
-        st1(1, 3, 0)
-        sig1(1, 3)
-        prod(3)
-        sig1(1, 0)
-        sig1(1, 1)
-        ln1(0, 0)
-        prod(1)
-        ln1(0, 1)
-        clamp(0, 0)
-        clamp(0, 1)
-        ln1(1, 0)
-        clamp(0, 3)
-        w2t(1, 0)
-        clamp(0, 2)
-        ln1(1, 1)
-        clamp(1, 1)
-        w2t(0, 0)
-        clamp(1, 0)
-        ln2(0, 0)
-        clamp(1, 2)
-        w2t(2, 0)
-        clamp(1, 3)
-        ln2(1, 0)
-        prod(2)
-        w2t(3, 0)
-        ln2(0, 1)
-        ln2(1, 1)
-        w2v(3, 0)
-        w2v(0, 0)
-        sig2(0)
-        q2(3, 0)
-        w2t(0, 1)
-        w2v(1, 0)
-        w2v(2, 0)
-        w2t(3, 1)
-        w2v(0, 1)
-        q2(0, 0)
-        w2t(2, 1)
-        consts()
-        q2(0, 1)
-        q2(1, 0)
-        w2t(1, 1)
-        sig2(1)
-        rat(0)
-        w2c(3, 1)
-        w2c(1, 1)
-        q2(2, 0)
-        plv(0, 2)
-        pls(0, 3)
-        wrap()
-        plv(0, 1)
-        wv(0, 2, 1)
-        rat(1)
-        wv(0, 3, 1)
-        wvc(0, 2, 1)
-        w2c(2, 1)
-        wv(0, 3, 0)
-        wvc(0, 3, 1)
-        wv(0, 1, 1)
-        wvc(0, 3, 0)
-        plv(0, 0)
-        wv(0, 1, 0)
-        wvc(0, 1, 1)
-        pls(1, 3)
-        wv(0, 2, 0)
-        dirv(0, 0)
-        wvc(0, 1, 0)
-        wv(1, 3, 0)
-        plv(1, 1)
-        wvc(0, 2, 0)
-        pls(1, 2)
-        qe(0, 0)
-        wv(1, 1, 0)
-        plv(1, 0)
-        st2(0, 0)
-        pls(2, 3)
-        q2(1, 1)
-        qe(0, 1)
-        wv(1, 2, 0)
-        q2(2, 1)
-        wvc(1, 1, 0)
-        st2(0, 1)
-        qe(0, 2)
-        wvc(1, 3, 0)
-        dirv(1, 0)
-        wvc(1, 2, 0)
-        st2(0, 2)
-        qe(0, 3)
-        pls(2, 2)
-        q2(3, 1)
-        st2(0, 3)
-        qe(1, 3)
-        qe(1, 0)
-        exps(0, 0)
-        plv(2, 1)
-        wv(2, 3, 0)
-        qe(1, 2)
-        wv(2, 2, 0)
-        plv(2, 0)
-        wv(2, 1, 0)
-        qe(1, 1)
-        dirv(2, 0)
-        exps(0, 1)
-        st2(1, 0)
-        fin(0, 0)
-        wvc(2, 2, 0)
-        fin(0, 1)
-        sto(0, 0)
-        st2(1, 1)
-        wvc(2, 3, 0)
-        st2(1, 2)
-        wvc(2, 1, 0)
-        qe(2, 0)
-        st2(1, 3)
-        sto(0, 1)
-        exps(1, 0)
-        qe(2, 1)
-        st2(2, 0)
-        qe(2, 2)
-        exps(1, 1)
-        qe(2, 3)
-        st2(2, 1)
-        fin(1, 0)
-        st2(2, 2)
-        fin(1, 1)
-        sto(1, 0)
-        st2(2, 3)
-        exps(2, 0)
-        sto(1, 1)
-        exps(2, 1)
-        fin(2, 0)
-        fin(2, 1)
-        sto(2, 0)
-        sto(2, 1)
+        stage1(0, 0, 0)
+        for quarter in range(2):
+            hg_tensor(1, 2, quarter, 4 + quarter)
+            hg_interleave(1, 2, quarter)
+        stage1(0, 1, 0)
+        hg_tensor(1, 3, 0, 6)
+        hg_interleave(1, 3, 0)
+        quantize_w("w1", w1_q, 0, 1)
+        hg_vector(1, 0)
+        for tap in range(1, TAPS):
+            quantize_w("w1", w1_q, tap, 1)
+        hg_vector(1, 1)
+        stage1(0, 2, 0)
+        stage1(0, 3, 0)
+        for tap in range(TAPS):
+            stage1(0, tap, 1)
+        sigmoid_s(0)
+        hg_tensor(1, 3, 1, 7)
+        log(0, 1.0)
+        hg_interleave(1, 3, 1)
+        quantize_hg(1, 0)
+        scale_w2(0)
+        quantize_hg(1, 1)
+        scale_w2(1)
+        clamp(0)
+        log(0, -4.0)
+        sigmoid_log(0)
+        quantize_hg(1, 2)
+        scale_w2(2)
+        quantize_hg(1, 3)
+        scale_w2(3)
+        second_constants()
+
+        for tap in range(TAPS):
+            stage1(1, tap, 0)
+            stage1(1, tap, 1)
+        sigmoid_s(1)
+        turn_w2(0, 0)
+        turn_w2(1, 0)
+        log(1, 1.0)
+        turn_w2(2, 0)
+        turn_w2(3, 0)
+        make_ratio(0)
+        quantize_w("w2", w2_q, 0, 0)
+        eg_vector(0, 0)
+        eg_vector(0, 1)
+        clamp(1)
+        log(1, -4.0)
+        turn_w2(0, 1)
+        turn_w2(1, 1)
+        sigmoid_log(1)
+        turn_w2(2, 1)
+        turn_w2(3, 1)
+        wrap_ratio()
+        eg_vector(0, 2)
+        quantize_eg(0, 0)
+        quantize_w("w2", w2_q, 1, 0)
+        eg_vector(0, 3)
+        quantize_eg(0, 1)
+        quantize_w("w2", w2_q, 2, 0)
+        quantize_w("w2", w2_q, 3, 0)
+        quantize_eg(0, 2)
+        quantize_w("w2", w2_q, 0, 1)
+        quantize_w("w2", w2_q, 1, 1)
+        quantize_eg(0, 3)
+
+        make_ratio(1)
+        quantize_w("w2", w2_q, 2, 1)
+        eg_vector(1, 0)
+        quantize_w("w2", w2_q, 3, 1)
+        stage2(0, 0)
+        eg_scalar(1, SCALAR_TAP)
+        eg_vector(1, 1)
+        quantize_eg(1, 0)
+        eg_vector(1, 2)
+        quantize_eg(1, 1)
+        exponential(0, 0)
+        exponential(0, 1)
+        eg_scalar(2, SCALAR_TAP)
+        eg_vector(2, 0)
+        quantize_eg(1, 2)
+        eg_vector(2, 1)
+        quantize_eg(1, 3)
+        stage2(1, 0)
+        eg_vector(2, 2)
+        finish(0, 0)
+        finish(0, 1)
+        quantize_eg(2, 0)
+        quantize_eg(2, 1)
+        exponential(1, 0)
+        exponential(1, 1)
+        finish(1, 0)
+        quantize_eg(2, 2)
+        quantize_eg(2, 3)
+        stage2(2, 4)
+        finish(1, 1)
+        for pair in range(2):
+            exponential(2, pair)
+            finish(2, pair)

@@ -23,6 +23,7 @@ TINY = 2.0 ** -60
 FLOPS = 2 * 2 * F * TAPS * K * T
 
 CHUNKS = ((0, (256, 128)), (384, (256, 128)), (768, (256,)))
+WIDEST = 384
 SCALAR_TAP = 3
 
 
@@ -74,6 +75,8 @@ def tile_convolutivenmfexponentiatedupdate_kernel(tc, v, h, w1, g1, w2_bytes, w2
         nc.vector.memset(dummy[:], 0.0)
         nc.scalar.activation(out=dummy[:, 1:2], in_=dummy[:, 0:1], func=ACT.Sigmoid)
 
+        g1_neg32 = keep.tile([P, TAPS, J], F32, name="g1_neg32")
+        nc.vector.tensor_scalar(out=g1_neg32[:], in0=g1_sb[:, :, 0:J], scalar1=-1.0, scalar2=None, op0=ALU.mult)
         g1_neg = keep.tile([P, TAPS, J], BF16, name="g1_neg")
         nc.vector.tensor_scalar(out=g1_neg[:], in0=g1_sb[:, :, 0:J], scalar1=-1.0, scalar2=None, op0=ALU.mult)
         g2_neg = keep.tile([P, TAPS, J], F32, name="g2_neg")
@@ -96,7 +99,7 @@ def tile_convolutivenmfexponentiatedupdate_kernel(tc, v, h, w1, g1, w2_bytes, w2
         hg_q, w1_q, eg_q, w2_q = operand("hg", T), operand("w1", F), operand("eg", T), operand("w2", K)
         h_il = keep.tile([P, PAD + T, J], BF16, name="h_il", align_bytes=64)
         diag = keep.tile([P, TAPS, J, P], BF16, name="diag")
-        act = keep.tile([P, BLOCKS, T], F32, name="act", align_bytes=64)
+        act = [keep.tile([P, BLOCKS, HALF], F32, name="act%d" % n, align_bytes=64) for n in range(2)]
         ratio = keep.tile([P, T + TAPS, J], F32, name="ratio", align_bytes=64)
 
         def quantize(operand_q, tap, lo, width, grouped):
@@ -157,16 +160,15 @@ def tile_convolutivenmfexponentiatedupdate_kernel(tc, v, h, w1, g1, w2_bytes, w2
 
         def make_diag(tap):
             for j in range(J):
-                nc.vector.tensor_scalar(
-                    out=diag[:, tap, j, :], in0=ident16[:], scalar1=g1_neg[:, tap, j : j + 1], scalar2=None, op0=ALU.mult
-                )
+                nc.scalar.activation(out=diag[:, tap, j, :], in_=ident16[:], func=ACT.Copy, scale=g1_neg32[:, tap, j : j + 1])
 
-        def hg_vector(n, tap):
-            lo = PAD + n * HALF - tap
+        def hg_vector(n, tap, first=0):
+            tile = grouped_tile(("hg", n, tap)) if first == 0 else grouped["hg", n, tap]
+            lo, hi = PAD + n * HALF + first - tap, PAD + (n + 1) * HALF - tap
             nc.vector.tensor_tensor(
-                out=grouped_tile(("hg", n, tap))[:],
-                in0=h_il[:, lo : lo + HALF, :],
-                in1=g1_neg[:, tap, :].unsqueeze(1).to_broadcast([P, HALF, J]),
+                out=tile[:, first:HALF, :],
+                in0=h_il[:, lo:hi, :],
+                in1=g1_neg[:, tap, :].unsqueeze(1).to_broadcast([P, hi - lo, J]),
                 op=ALU.mult,
             )
 
@@ -202,25 +204,25 @@ def tile_convolutivenmfexponentiatedupdate_kernel(tc, v, h, w1, g1, w2_bytes, w2
 
         def sigmoid_s(n):
             for b in range(BLOCKS):
-                nc.scalar.activation(out=act[:, b, half(n)], in_=s_banks[n, b][:], func=ACT.Sigmoid)
+                nc.scalar.activation(out=act[n][:, b, :], in_=s_banks[n, b][:], func=ACT.Sigmoid)
 
         def log(n, scale):
             for pair in range(2):
-                part = act[:, 2 * pair : 2 * pair + 2, half(n)]
+                part = act[n][:, 2 * pair : 2 * pair + 2, :]
                 nc.scalar.activation(out=part, in_=part, func=ACT.Ln, scale=scale, bias=TINY)
 
         def clamp(n):
             for b in range(BLOCKS):
-                part = act[:, b, half(n)]
+                part = act[n][:, b, :]
                 nc.vector.scalar_tensor_tensor(out=part, in0=s_banks[n, b][:], scalar=0.0, in1=part, op0=ALU.min, op1=ALU.min)
 
         def sigmoid_log(n):
-            nc.scalar.activation(out=act[:, :, half(n)], in_=act[:, :, half(n)], func=ACT.Sigmoid, scale=-1.0)
+            nc.scalar.activation(out=act[n][:], in_=act[n][:], func=ACT.Sigmoid, scale=-1.0)
 
         def make_ratio(n):
             nc.vector.tensor_tensor(
                 out=ratio[:, half(n), :].rearrange("p (c i) b -> p c b i", i=4),
-                in0=act[:, :, half(n)].rearrange("p b (c i) -> p c b i", i=4),
+                in0=act[n][:].rearrange("p b (c i) -> p c b i", i=4),
                 in1=v_sb[:, :, half(n)].rearrange("p b (c i) -> p c b i", i=4),
                 op=ALU.mult,
             )
@@ -257,7 +259,7 @@ def tile_convolutivenmfexponentiatedupdate_kernel(tc, v, h, w1, g1, w2_bytes, w2
 
         def eg_scalar(c, tap):
             lo, hi = columns(c)
-            rows = stage.tile([P, J, HALF], BF16, name="eg_rows", align_bytes=64, bufs=2)
+            rows = stage.tile([P, J, WIDEST], BF16, name="eg_rows", align_bytes=64, bufs=2)
             for j in range(J):
                 nc.scalar.activation(
                     out=rows[:, j, 0 : hi - lo],
@@ -293,7 +295,7 @@ def tile_convolutivenmfexponentiatedupdate_kernel(tc, v, h, w1, g1, w2_bytes, w2
 
         def exponential(c, pair):
             lo, hi = columns(c)
-            grown[c, pair] = stage.tile([P, 2, HALF], F32, name="grown")
+            grown[c, pair] = stage.tile([P, 2, WIDEST], F32, name="grown")
             for b in range(2):
                 block = 2 * pair + b
                 nc.scalar.activation(
@@ -309,7 +311,7 @@ def tile_convolutivenmfexponentiatedupdate_kernel(tc, v, h, w1, g1, w2_bytes, w2
         def finish(c, pair):
             lo, hi = columns(c)
             rows = slice(2 * pair, 2 * pair + 2)
-            result = stage.tile([P, 2, HALF], F32, name="result")
+            result = stage.tile([P, 2, WIDEST], F32, name="result", bufs=6)
             nc.vector.tensor_tensor(
                 out=result[:, :, 0 : hi - lo],
                 in0=grown[c, pair][:, :, 0 : hi - lo],
@@ -322,9 +324,9 @@ def tile_convolutivenmfexponentiatedupdate_kernel(tc, v, h, w1, g1, w2_bytes, w2
                     nc.sync.dma_start(out=out_rows[:, rows, time : time + z - a], in_=result[:, :, a - lo : z - lo])
 
         make_diag(3)
+        make_diag(2)
         interleave_h(nc.vector.tensor_copy, PAD - TAPS, PAD + QUARTER)
         interleave_h(nc.vector.tensor_copy, PAD + QUARTER, PAD + HALF)
-        make_diag(2)
         for quarter in range(2):
             hg_tensor(0, 3, quarter, 2 + quarter)
             hg_interleave(0, 3, quarter)
@@ -345,57 +347,61 @@ def tile_convolutivenmfexponentiatedupdate_kernel(tc, v, h, w1, g1, w2_bytes, w2
         for tap in range(TAPS):
             turn("w1", w1_sb[:], tap, 1, 4 + tap)
             empty("w1", tap, 1)
-            if tap % 2 == 1:
+            if tap == 1:
                 warm()
         interleave_h(nc.vector.tensor_copy, PAD + HALF + QUARTER, PAD + T)
         for tap in range(3):
             quantize_hg(0, tap)
 
-        stage1(0, 0, 0)
         for quarter in range(2):
             hg_tensor(1, 2, quarter, 4 + quarter)
             hg_interleave(1, 2, quarter)
+        stage1(0, 0, 0)
         stage1(0, 1, 0)
         hg_tensor(1, 3, 0, 6)
         hg_interleave(1, 3, 0)
+        stage1(0, 2, 0)
+        stage1(0, 3, 0)
         quantize_w("w1", w1_q, 0, 1)
+        stage1(0, 0, 1)
         hg_vector(1, 0)
         for tap in range(1, TAPS):
             quantize_w("w1", w1_q, tap, 1)
-        hg_vector(1, 1)
-        stage1(0, 2, 0)
-        stage1(0, 3, 0)
-        for tap in range(TAPS):
             stage1(0, tap, 1)
         sigmoid_s(0)
-        hg_tensor(1, 3, 1, 7)
-        log(0, 1.0)
-        hg_interleave(1, 3, 1)
+        hg_vector(1, 1)
         quantize_hg(1, 0)
+        stage1(1, 0, 0)
+        log(0, 1.0)
         scale_w2(0)
         quantize_hg(1, 1)
         scale_w2(1)
-        clamp(0)
-        log(0, -4.0)
-        sigmoid_log(0)
         quantize_hg(1, 2)
+        clamp(0)
+        hg_vector(1, 3, QUARTER)
+        log(0, -4.0)
+        stage1(1, 0, 1)
+        stage1(1, 1, 0)
+        stage1(1, 1, 1)
+        stage1(1, 2, 0)
+        stage1(1, 2, 1)
         scale_w2(2)
         quantize_hg(1, 3)
+        stage1(1, 3, 0)
+        stage1(1, 3, 1)
+        sigmoid_log(0)
+        sigmoid_s(1)
         scale_w2(3)
         second_constants()
 
-        for tap in range(TAPS):
-            stage1(1, tap, 0)
-            stage1(1, tap, 1)
-        sigmoid_s(1)
         turn_w2(0, 0)
         turn_w2(1, 0)
         log(1, 1.0)
         turn_w2(2, 0)
         turn_w2(3, 0)
         make_ratio(0)
-        quantize_w("w2", w2_q, 0, 0)
         eg_vector(0, 0)
+        quantize_w("w2", w2_q, 0, 0)
         eg_vector(0, 1)
         clamp(1)
         log(1, -4.0)
@@ -435,17 +441,17 @@ def tile_convolutivenmfexponentiatedupdate_kernel(tc, v, h, w1, g1, w2_bytes, w2
         eg_vector(2, 1)
         quantize_eg(1, 3)
         stage2(1, 0)
+        quantize_eg(2, 0)
         eg_vector(2, 2)
+        quantize_eg(2, 1)
         finish(0, 0)
         finish(0, 1)
-        quantize_eg(2, 0)
-        quantize_eg(2, 1)
+        quantize_eg(2, 3)
+        quantize_eg(2, 2)
+        stage2(2, 4)
         exponential(1, 0)
         exponential(1, 1)
         finish(1, 0)
-        quantize_eg(2, 2)
-        quantize_eg(2, 3)
-        stage2(2, 4)
         finish(1, 1)
         for pair in range(2):
             exponential(2, pair)

from contextlib import ExitStack

import concourse.mybir as mybir
from concourse.masks import make_identity

F32 = mybir.dt.float32
BF16 = mybir.dt.bfloat16
U32 = mybir.dt.uint32
U8 = mybir.dt.uint8
FP8 = mybir.dt.float8_e4m3fn
FP8X4 = mybir.dt.float8_e4m3fn_x4
ALU = mybir.AluOpType
ACT = mybir.ActivationFunctionType

F, K, T, TAPS = 512, 512, 1024, 4
P = 128
J = 4
BLOCKS = 4
HALF = T // 2
QUARTER = T // 4
PAD = 16
TINY = 2.0 ** -60
FLOPS = 2 * 2 * F * TAPS * K * T

CHUNKS = ((0, (256, 128)), (384, (256, 128)), (768, (256,)))
WIDEST = 384
SCALAR_TAP = 3


def tile_convolutivenmfexponentiatedupdate_kernel(tc, v, h, w1, g1, w2_bytes, w2_scale, g2, mu, out):
    nc = tc.nc
    with ExitStack() as ctx:
        ctx.enter_context(tc.manual_schedule())
        keep = ctx.enter_context(tc.tile_pool(name="keep", bufs=1))
        stage = ctx.enter_context(tc.tile_pool(name="stage", bufs=4))
        psum = ctx.enter_context(tc.psum_pool(name="psum", bufs=1))

        def bank(i, shape=(P, HALF), dtype=F32):
            return psum.tile(list(shape), dtype, name="bank%d" % i, tag="bank%d" % i)

        h_sb = keep.tile([P, J, PAD + T], BF16, name="h_sb", align_bytes=64)
        w1_sb = keep.tile([P, J, TAPS * K], BF16, name="w1_sb", tag="weight_rows", align_bytes=64)
        v_sb = keep.tile([P, J, T], BF16, name="v_sb")
        w2_codes_in = keep.tile([P, J, TAPS * F], U8, name="w2_codes_in", align_bytes=64)
        w2_scale_sb = keep.tile([P, TAPS * F], F32, name="w2_scale_sb", align_bytes=64)
        g1_sb = keep.tile([P, TAPS, 16], BF16, name="g1_sb")
        g2_sb = keep.tile([P, TAPS, 16], BF16, name="g2_sb")
        mu_sb = keep.tile([P, 16], BF16, name="mu_sb")
        h_rows = h.rearrange("(p j) t -> p j t", j=J)
        v_rows = v.rearrange("(p j) t -> p j t", j=J)
        w1_rows = w1.rearrange("(m b) k -> m b k", b=BLOCKS)
        w2_rows = w2_bytes.rearrange("(m b) k -> m b k", b=BLOCKS)
        nc.scalar.dma_start(out=g1_sb[:, :, 0:J], in_=g1.rearrange("(a p j) -> p a j", a=TAPS, j=J))
        mid = PAD + QUARTER
        nc.sync.dma_start(out=h_sb[:, :, PAD - TAPS : mid], in_=h_rows[:, :, HALF - TAPS : HALF + QUARTER])
        nc.sync.dma_start(out=h_sb[:, :, mid : PAD + HALF], in_=h_rows[:, :, HALF + QUARTER : T])
        for b in range(0, BLOCKS, 2):
            nc.sync.dma_start(out=w1_sb[:, b : b + 2, :], in_=w1_rows[:, b : b + 2, :])
        nc.sync.dma_start(out=h_sb[:, :, PAD + HALF : PAD + T], in_=h_rows[:, :, 0:HALF])
        nc.sync.dma_start(out=w2_codes_in[:, 0:2, :], in_=w2_rows[:, 0:2, :])
        nc.sync.dma_start(out=w2_scale_sb[:], in_=w2_scale.rearrange("o k -> (o k)").partition_broadcast(P))
        nc.sync.dma_start(out=w2_codes_in[:, 2:4, :], in_=w2_rows[:, 2:4, :])
        nc.sync.dma_start(out=v_sb[:, :, 0:HALF], in_=v_rows[:, :, HALF:T])
        nc.sync.dma_start(out=v_sb[:, :, HALF:T], in_=v_rows[:, :, 0:HALF])
        nc.sync.dma_start(out=g2_sb[:, :, 0:J], in_=g2.rearrange("(a p j) -> p a j", a=TAPS, j=J))
        nc.sync.dma_start(out=mu_sb[:, 0:J], in_=mu.rearrange("(p j) -> p j", j=J))

        ident = keep.tile([P, P], F32, name="ident")
        make_identity(nc, ident[:])
        ident16 = keep.tile([P, P], BF16, name="ident16")
        make_identity(nc, ident16[:])
        zeros = keep.tile([P, QUARTER], F32, name="zeros")
        nc.gpsimd.memset(zeros[:], 0.0)
        dummy = keep.tile([P, 2], F32, name="dummy")
        nc.vector.memset(dummy[:], 0.0)
        nc.scalar.activation(out=dummy[:, 1:2], in_=dummy[:, 0:1], func=ACT.Sigmoid)

        g1_neg32 = keep.tile([P, TAPS, J], F32, name="g1_neg32")
        nc.vector.tensor_scalar(out=g1_neg32[:], in0=g1_sb[:, :, 0:J], scalar1=-1.0, scalar2=None, op0=ALU.mult)
        g1_neg = keep.tile([P, TAPS, J], BF16, name="g1_neg")
        nc.vector.tensor_scalar(out=g1_neg[:], in0=g1_sb[:, :, 0:J], scalar1=-1.0, scalar2=None, op0=ALU.mult)
        g2_neg = keep.tile([P, TAPS, J], F32, name="g2_neg")
        g2_four = keep.tile([P, TAPS, J], F32, name="g2_four")
        g2_four16 = keep.tile([P, TAPS, J], BF16, name="g2_four16")
        mu_half = keep.tile([P, J], F32, name="mu_half")

        def second_constants():
            nc.vector.tensor_scalar(out=mu_half[:], in0=mu_sb[:, 0:J], scalar1=-0.5, scalar2=None, op0=ALU.mult)
            nc.vector.tensor_scalar(out=g2_neg[:], in0=g2_sb[:, :, 0:J], scalar1=-1.0, scalar2=None, op0=ALU.mult)
            nc.vector.tensor_scalar(out=g2_four16[:], in0=g2_sb[:, :, 0:J], scalar1=4.0, scalar2=None, op0=ALU.mult)
            nc.vector.tensor_scalar(out=g2_four[:], in0=g2_sb[:, :, 0:J], scalar1=4.0, scalar2=None, op0=ALU.mult)

        def operand(name, width):
            return (
                keep.tile([P, TAPS, width], U32, name=name + "_codes", align_bytes=64),
                keep.tile([P, TAPS, width], U8, name=name + "_scales", align_bytes=64),
            )

        hg_q, w1_q, eg_q, w2_q = operand("hg", T), operand("w1", F), operand("eg", T), operand("w2", K)
        h_il = keep.tile([P, PAD + T, J], BF16, name="h_il", align_bytes=64)
        diag = keep.tile([P, TAPS, J, P], BF16, name="diag")
        act = [keep.tile([P, BLOCKS, HALF], F32, name="act%d" % n, align_bytes=64) for n in range(2)]
        ratio = keep.tile([P, T + TAPS, J], F32, name="ratio", align_bytes=64)

        def quantize(operand_q, tap, lo, width, grouped):
            codes, scales = operand_q
            nc.vector.quantize_mx(
                out=codes[:, tap, lo : lo + width].bitcast(FP8X4),
                scales=scales[:, tap, lo : lo + width],
                in_=grouped.rearrange("p c j -> p (c j)"),
            )

        def multiply(ps, weight_q, moving_q, b, tap, lo, width):
            rows, columns = slice(b * P, (b + 1) * P), slice(lo, lo + width)
            nc.tensor.matmul_mx(
                out=ps,
                lhsT=weight_q[0][:, tap, rows].bitcast(FP8X4),
                lhsT_scale=weight_q[1][:, tap, rows],
                rhs=moving_q[0][:, tap, columns].bitcast(FP8X4),
                rhs_scale=moving_q[1][:, tap, columns],
                start=(tap == 0),
                stop=(tap == TAPS - 1),
            )

        def warm():
            nc.tensor.matmul(bank(0)[:, 0:QUARTER], lhsT=ident[:], rhs=zeros[:], start=True, stop=True)

        turned, grouped_w = {}, {}

        def turn(name, rows_sb, tap, pair, i):
            words = rows_sb.bitcast(F32)
            ps = bank(i, (P, 2, 2, P))
            for b in range(2):
                for u in range(2):
                    start = tap * (K // 2) + u
                    nc.tensor.transpose(ps[:, b, u, :], words[:, 2 * pair + b, start : (tap + 1) * (K // 2) : 2], ident[:])
            turned[name, tap, pair] = ps

        def empty(name, tap, pair):
            if (name, tap) not in grouped_w:
                grouped_w[name, tap] = stage.tile([P, BLOCKS * P, J], BF16, name="grouped_w", align_bytes=64)
            part = grouped_w[name, tap][:, pair * 2 * P : (pair + 1) * 2 * P, :].rearrange("p m j -> p (m j)").bitcast(F32)
            nc.scalar.copy(
                out=part.rearrange("p (b m u) -> p b m u", b=2, u=2),
                in_=turned[name, tap, pair][:].rearrange("p b u m -> p b m u"),
            )

        def quantize_w(name, weight_q, tap, pair):
            lo = pair * 2 * P
            quantize(weight_q, tap, lo, 2 * P, grouped_w[name, tap][:, lo : lo + 2 * P, :])

        grouped = {}

        def grouped_tile(key):
            grouped[key] = stage.tile([P, HALF, J], BF16, name="grouped", align_bytes=64, bufs=6)
            return grouped[key]

        def interleave_h(copy, lo, hi):
            copy(out=h_il[:, lo:hi, :], in_=h_sb[:, :, lo:hi].rearrange("p j t -> p t j"))

        def make_diag(tap):
            for j in range(J):
                nc.scalar.activation(out=diag[:, tap, j, :], in_=ident16[:], func=ACT.Copy, scale=g1_neg32[:, tap, j : j + 1])

        def hg_vector(n, tap, first=0):
            tile = grouped_tile(("hg", n, tap)) if first == 0 else grouped["hg", n, tap]
            lo, hi = PAD + n * HALF + first - tap, PAD + (n + 1) * HALF - tap
            nc.vector.tensor_tensor(
                out=tile[:, first:HALF, :],
                in0=h_il[:, lo:hi, :],
                in1=g1_neg[:, tap, :].unsqueeze(1).to_broadcast([P, hi - lo, J]),
                op=ALU.mult,
            )

        hg_banks = {}

        def hg_tensor(n, tap, quarter, i):
            lo = PAD + n * HALF + quarter * QUARTER - tap
            ps = bank(i, (P, J, QUARTER), BF16)
            for j in range(J):
                nc.tensor.matmul(ps[:, j, :], lhsT=diag[:, tap, j, :], rhs=h_sb[:, j, lo : lo + QUARTER], start=True, stop=True)
            hg_banks[n, tap, quarter] = ps

        def hg_interleave(n, tap, quarter):
            tile = grouped_tile(("hg", n, tap)) if quarter == 0 else grouped["hg", n, tap]
            nc.scalar.copy(
                out=tile[:, quarter * QUARTER : (quarter + 1) * QUARTER, :],
                in_=hg_banks[n, tap, quarter][:].rearrange("p j t -> p t j"),
            )

        def quantize_hg(n, tap):
            quantize(hg_q, tap, n * HALF, HALF, grouped["hg", n, tap][:])

        s_banks = {}

        def stage1(n, tap, pair):
            for b in range(2 * pair, 2 * pair + 2):
                if tap == 0:
                    s_banks[n, b] = bank(n * BLOCKS + b)
                multiply(s_banks[n, b][:], w1_q, hg_q, b, tap, n * HALF, HALF)

        def half(n):
            return slice(n * HALF, (n + 1) * HALF)

        def sigmoid_s(n):
            for b in range(BLOCKS):
                nc.scalar.activation(out=act[n][:, b, :], in_=s_banks[n, b][:], func=ACT.Sigmoid)

        def log(n, scale):
            for pair in range(2):
                part = act[n][:, 2 * pair : 2 * pair + 2, :]
                nc.scalar.activation(out=part, in_=part, func=ACT.Ln, scale=scale, bias=TINY)

        def clamp(n):
            for b in range(BLOCKS):
                part = act[n][:, b, :]
                nc.vector.scalar_tensor_tensor(out=part, in0=s_banks[n, b][:], scalar=0.0, in1=part, op0=ALU.min, op1=ALU.min)

        def sigmoid_log(n):
            nc.scalar.activation(out=act[n][:], in_=act[n][:], func=ACT.Sigmoid, scale=-1.0)

        def make_ratio(n):
            nc.vector.tensor_tensor(
                out=ratio[:, half(n), :].rearrange("p (c i) b -> p c b i", i=4),
                in0=act[n][:].rearrange("p b (c i) -> p c b i", i=4),
                in1=v_sb[:, :, half(n)].rearrange("p b (c i) -> p c b i", i=4),
                op=ALU.mult,
            )

        def wrap_ratio():
            nc.vector.tensor_copy(out=ratio[:, T : T + TAPS - 1, :], in_=ratio[:, 0 : TAPS - 1, :])

        w2_sb = []

        def scale_w2(b):
            if not w2_sb:
                w2_sb.append(keep.tile([P, J, TAPS * F], BF16, name="w2_sb", tag="weight_rows", align_bytes=64))
            nc.vector.tensor_tensor(
                out=w2_sb[0][:, b, :], in0=w2_codes_in[:, b, :].bitcast(FP8), in1=w2_scale_sb[:], op=ALU.mult
            )

        def turn_w2(tap, pair):
            turn("w2", w2_sb[0][:], tap, pair, tap % 2)
            empty("w2", tap, pair)

        def columns(c):
            return CHUNKS[c][0], CHUNKS[c][0] + sum(CHUNKS[c][1])

        def eg_vector(c, tap):
            lo, hi = columns(c)
            nc.vector.scalar_tensor_tensor(
                out=grouped_tile(("eg", c, tap))[:, 0 : hi - lo, :],
                in0=ratio[:, lo + tap : hi + tap, :],
                scalar=0.25,
                in1=g2_four16[:, tap, :].unsqueeze(1).to_broadcast([P, hi - lo, J]),
                op0=ALU.subtract,
                op1=ALU.mult,
            )

        def eg_scalar(c, tap):
            lo, hi = columns(c)
            rows = stage.tile([P, J, WIDEST], BF16, name="eg_rows", align_bytes=64, bufs=2)
            for j in range(J):
                nc.scalar.activation(
                    out=rows[:, j, 0 : hi - lo],
                    in_=ratio[:, lo + tap : hi + tap, j],
                    func=ACT.Identity,
                    scale=g2_four[:, tap, j : j + 1],
                    bias=g2_neg[:, tap, j : j + 1],
                )
            nc.scalar.copy(out=grouped_tile(("eg", c, tap))[:, 0 : hi - lo, :], in_=rows[:, :, 0 : hi - lo].rearrange("p j t -> p t j"))

        def pieces(c):
            lo, list_of_pieces = CHUNKS[c][0], []
            for width in CHUNKS[c][1]:
                list_of_pieces.append((lo, width))
                lo += width
            return list_of_pieces

        def quantize_eg(c, tap):
            first = CHUNKS[c][0]
            for lo, width in pieces(c):
                quantize(eg_q, tap, lo, width, grouped["eg", c, tap][:, lo - first : lo - first + width, :])

        r_banks, grown = {}, {}

        def stage2(c, first_bank):
            first = CHUNKS[c][0]
            for b in range(BLOCKS):
                r_banks[c, b] = bank(first_bank + b)
            for lo, width in pieces(c):
                for tap in range(TAPS):
                    for b in range(BLOCKS):
                        multiply(r_banks[c, b][:, lo - first : lo - first + width], w2_q, eg_q, b, tap, lo, width)

        def exponential(c, pair):
            lo, hi = columns(c)
            grown[c, pair] = stage.tile([P, 2, WIDEST], F32, name="grown")
            for b in range(2):
                block = 2 * pair + b
                nc.scalar.activation(
                    out=grown[c, pair][:, b, 0 : hi - lo],
                    in_=r_banks[c, block][:, 0 : hi - lo],
                    func=ACT.Exp,
                    scale=0.5,
                    bias=mu_half[:, block : block + 1],
                )

        out_rows = out.rearrange("(p b) t -> p b t", b=BLOCKS)

        def finish(c, pair):
            lo, hi = columns(c)
            rows = slice(2 * pair, 2 * pair + 2)
            result = stage.tile([P, 2, WIDEST], F32, name="result", bufs=6)
            nc.vector.tensor_tensor(
                out=result[:, :, 0 : hi - lo],
                in0=grown[c, pair][:, :, 0 : hi - lo],
                in1=h_sb[:, rows, PAD + lo : PAD + hi],
                op=ALU.mult,
            )
            for a, z in ((lo, min(hi, HALF)), (max(lo, HALF), hi)):
                if a < z:
                    time = (a + HALF) % T
                    nc.sync.dma_start(out=out_rows[:, rows, time : time + z - a], in_=result[:, :, a - lo : z - lo])

        make_diag(3)
        make_diag(2)
        interleave_h(nc.vector.tensor_copy, PAD - TAPS, PAD + QUARTER)
        interleave_h(nc.vector.tensor_copy, PAD + QUARTER, PAD + HALF)
        for quarter in range(2):
            hg_tensor(0, 3, quarter, 2 + quarter)
            hg_interleave(0, 3, quarter)
        warm()
        hg_vector(0, 0)
        hg_vector(0, 1)
        for tap in range(TAPS):
            turn("w1", w1_sb[:], tap, 0, 4 + tap)
            empty("w1", tap, 0)
            if tap % 2 == 1:
                warm()
        quantize_hg(0, 3)
        quantize_w("w1", w1_q, 0, 0)
        hg_vector(0, 2)
        for tap in range(1, TAPS):
            quantize_w("w1", w1_q, tap, 0)
        interleave_h(nc.scalar.copy, PAD + HALF, PAD + HALF + QUARTER)
        for tap in range(TAPS):
            turn("w1", w1_sb[:], tap, 1, 4 + tap)
            empty("w1", tap, 1)
            if tap == 1:
                warm()
        interleave_h(nc.vector.tensor_copy, PAD + HALF + QUARTER, PAD + T)
        for tap in range(3):
            quantize_hg(0, tap)

        for quarter in range(2):
            hg_tensor(1, 2, quarter, 4 + quarter)
            hg_interleave(1, 2, quarter)
        stage1(0, 0, 0)
        stage1(0, 1, 0)
        hg_tensor(1, 3, 0, 6)
        hg_interleave(1, 3, 0)
        stage1(0, 2, 0)
        stage1(0, 3, 0)
        quantize_w("w1", w1_q, 0, 1)
        stage1(0, 0, 1)
        hg_vector(1, 0)
        for tap in range(1, TAPS):
            quantize_w("w1", w1_q, tap, 1)
            stage1(0, tap, 1)
        sigmoid_s(0)
        hg_vector(1, 1)
        quantize_hg(1, 0)
        stage1(1, 0, 0)
        log(0, 1.0)
        scale_w2(0)
        quantize_hg(1, 1)
        scale_w2(1)
        quantize_hg(1, 2)
        clamp(0)
        hg_vector(1, 3, QUARTER)
        log(0, -4.0)
        stage1(1, 0, 1)
        stage1(1, 1, 0)
        stage1(1, 1, 1)
        stage1(1, 2, 0)
        stage1(1, 2, 1)
        scale_w2(2)
        quantize_hg(1, 3)
        stage1(1, 3, 0)
        stage1(1, 3, 1)
        sigmoid_log(0)
        sigmoid_s(1)
        scale_w2(3)
        second_constants()

        turn_w2(0, 0)
        turn_w2(1, 0)
        log(1, 1.0)
        turn_w2(2, 0)
        turn_w2(3, 0)
        make_ratio(0)
        eg_vector(0, 0)
        quantize_w("w2", w2_q, 0, 0)
        eg_vector(0, 1)
        clamp(1)
        log(1, -4.0)
        turn_w2(0, 1)
        turn_w2(1, 1)
        sigmoid_log(1)
        turn_w2(2, 1)
        turn_w2(3, 1)
        wrap_ratio()
        eg_vector(0, 2)
        quantize_eg(0, 0)
        quantize_w("w2", w2_q, 1, 0)
        eg_vector(0, 3)
        quantize_eg(0, 1)
        quantize_w("w2", w2_q, 2, 0)
        quantize_w("w2", w2_q, 3, 0)
        quantize_eg(0, 2)
        quantize_w("w2", w2_q, 0, 1)
        quantize_w("w2", w2_q, 1, 1)
        quantize_eg(0, 3)

        make_ratio(1)
        quantize_w("w2", w2_q, 2, 1)
        eg_vector(1, 0)
        quantize_w("w2", w2_q, 3, 1)
        stage2(0, 0)
        eg_scalar(1, SCALAR_TAP)
        eg_vector(1, 1)
        quantize_eg(1, 0)
        eg_vector(1, 2)
        quantize_eg(1, 1)
        exponential(0, 0)
        exponential(0, 1)
        eg_scalar(2, SCALAR_TAP)
        eg_vector(2, 0)
        quantize_eg(1, 2)
        eg_vector(2, 1)
        quantize_eg(1, 3)
        stage2(1, 0)
        quantize_eg(2, 0)
        eg_vector(2, 2)
        quantize_eg(2, 1)
        finish(0, 0)
        finish(0, 1)
        quantize_eg(2, 3)
        quantize_eg(2, 2)
        stage2(2, 4)
        exponential(1, 0)
        exponential(1, 1)
        finish(1, 0)
        finish(1, 1)
        for pair in range(2):
            exponential(2, pair)
            finish(2, pair)
